import numpy as np, ml_dtypes
CORES = [5,29,101,125,133,157,229,253]
N = 8
import mx_ref
BF = ml_dtypes.bfloat16
def entries(a):
    return np.ascontiguousarray(a.T).reshape(-1)
def table(e):
    return np.ascontiguousarray(np.reshape(e, (-1, 16)).T).astype(np.int32)
def cols(t, e):
    v = np.concatenate([t.reshape(128, -1, 4), np.zeros((128, 1, 4), BF)], axis=1)
    return np.ascontiguousarray(v[:, e]).reshape(128, -1)
def cut(t, i, w=512):
    return t[:, w * i:w * i + w]
def f(rng, *shape):
    return mx_ref.flush((rng.standard_normal(shape, dtype=np.float32) * np.exp2(rng.integers(-2, 3, shape[:-1] + (1,)))).astype(BF))
def wide(rng, *shape, cols=0):
    v = rng.standard_normal(shape, dtype=np.float32) * np.exp2(rng.integers(-12, 13, shape)).astype(np.float32)
    if cols: v *= np.repeat(np.exp2(rng.integers(-cols, cols + 1, shape[:-2] + (1, shape[-1] // 4))) * (rng.random(shape[:-2] + (1, shape[-1] // 4)) > 0.0625), 4, axis=-1).astype(np.float32)
    return mx_ref.flush(v.astype(BF))
C, P, B, O, DN, DS = 128, 256, 2, 2, 160, 80
def lists(rng, S, straddle=0.5, fill="any", flip=None):
    o = np.array([[max(0, min(S[r + 1], P * q + P) - max(S[r], P * q)) for q in range(N)] for r in range(N)])
    ends, both = np.zeros((N, N), int), {}
    for r in range(N):
        for q in range(N - 1):
            if o[r, q] > 0 and o[r, q + 1] > 0 and rng.random() < straddle:
                a = int(rng.integers(1, min(5, o[r, q]) + 1))
                b = int(rng.integers(1, min(6 - a, o[r, q + 1]) + 1))
                if fill == "few":
                    a = int(o[r, q] % 6); b = 6 - a
                    if a == 0: continue
                o[r, q] -= a; o[r, q + 1] -= b
                ends[r, q] += 1; ends[r, q + 1] += 1; both[r, q] = a + b
    K = np.floor_divide(o + 5, 6)
    segs = [(r, q) for r in range(N) for q in range(N) if o[r, q] > 0]
    segs = [segs[i] for i in rng.permutation(len(segs))]
    if fill == "full": segs = [s for s in segs if s[1] % 2 == 1] + [s for s in segs if s[1] % 2 == 0]
    if fill == "few": segs = []
    for r, q in segs:
        room = int(min(DS - ends[r, q] - K[r, q], o[r, q] - K[r, q], C - (ends[r].sum() >> 1) - K[r].sum(), DN - ends[:, q].sum() - K[:, q].sum()))
        K[r, q] += room if fill == "full" else rng.integers(0, room + 1)
    m = np.zeros((N, C), int)
    for r in range(N):
        e = []
        for q in range(N):
            k = int(K[r, q])
            e += (1 + np.bincount(rng.permutation(np.repeat(np.arange(k), 5))[:o[r, q] - k], minlength=k)).tolist()
            if (r, q) in both: e.append(both[r, q])
        m[r, np.sort(rng.permutation(C)[:len(e)])] = np.array(e, int)
    if flip is None: flip = rng.random() < 0.5
    if flip: m = m[::-1, ::-1]
    return {"cnt": np.stack([table(e) for e in m])}
def begins(rng):
    for k in range(50):
        S, e = [0], 1 - 2 * int(rng.integers(2))
        turn = N if rng.random() < 0.5 else int(rng.integers(2, N))
        for r in range(1, N):
            if r == turn: e = -e
            s = S[-1] - P * (r - 1)
            lo = max(s - P, -2 * P, -((3 * P * (N - r)) >> 1))
            hi = min(s + ((3 * P) >> 1), 2 * P, P * (N - r))
            a, b = (max(lo, (3 * P) >> 2), hi) if e > 0 else (lo, min(hi, -((3 * P) >> 2)))
            if a > b: a = b = hi if e > 0 else lo
            S.append(P * r + int(rng.integers(a, b + 1)))
        S.append(N * P)
        own = sum(max(0, min(S[r + 1], P * r + P) - max(S[r], P * r)) for r in range(N))
        if 2 * own <= N * P: return S
    raise RuntimeError("begins")
def floats(rng):
    return {"x": f(rng, N, 128, 4 * C), "w": f(rng, N, 128, 512 * B * O)}
def setup_inputs(rng):
    return {**floats(rng), **lists(rng, begins(rng))}
def setup_inputs_full(rng):
    S = [0] + [P * r + (P >> 1) + int(rng.integers(-(P >> 4), (P >> 4) + 1)) for r in range(1, N)] + [N * P]
    return {**floats(rng), **lists(rng, S, straddle=2.0, fill="full")}
def setup_inputs_furthest(rng):
    S = [0] + [min(P * (r + 2), N * P) for r in range(1, N + 1)]
    return {**floats(rng), **lists(rng, S, straddle=2.0, fill="few")}
def setup_inputs_dense(rng):
    def some(k, n):
        return (1 + np.bincount(rng.permutation(np.repeat(np.arange(k), 5))[:n - k], minlength=k)).tolist()
    H = min(P // 256 * 128 + 64, P - DS) if N > 4 else (P - 1) // 256 * 128 + 64
    X = (7 * DS - P) // 5
    flip = bool(rng.random() < 0.5)
    front = 3 + 2 * int(rng.integers((N - 2) // 2))
    e = [[] for r in range(N)]
    for q in range(2, N):
        h, i, j = P // 2, 0, 0
        if q == front: h, i, j = (P - DS, X, DS) if flip else (DS, DS, X)
        elif q % 2 == 1 or N == 4: h, i, j = H, H % 128, 128 - H % 128
        a, b = h - i, P - h - j
        if q == 2: a += 2 * P
        if q % 2 == 1: ka, kb = DS - i, DS - j
        else:
            ka = int(rng.integers(-(-a // 6), (C if q == 2 else C - DS) - i + 1))
            kb = int(rng.integers(-(-b // 6), C - DS - j + 1))
        e[q - 2] += some(ka, a) + [1] * i
        e[q - 1] += [1] * j + some(kb, b)
    m = np.zeros((N, C), int)
    for r in range(N):
        m[r, np.sort(rng.permutation(C)[:len(e[r])])] = np.array(e[r], int)
    if flip: m = m[::-1, ::-1]
    return {**floats(rng), "cnt": np.stack([table(v) for v in m])}
def setup_inputs_many(rng):
    def some(k, n):
        return (1 + np.bincount(rng.permutation(np.repeat(np.arange(k), 5))[:n - k], minlength=k)).tolist()
    src = [[0], [0, 1, 2, 3], [3], [3]] if N == 4 else [[0], [0], [0, 1, 2, 3, 4], [4], [4], [4, 5, 6, 7], [7], [7]]
    flip = bool(rng.random() < 0.5)
    lo = -(-P // 6)
    alone = [src.count([r]) for r in range(N)]
    among = [sum(len(s) > 1 and r in s for s in src) for r in range(N)]
    least = [alone[r] * lo + (1 - among[r] - alone[r] * lo) % N for r in range(N)]
    k = np.zeros((N, N), int)
    for q, s in enumerate(src):
        if len(s) == 1: continue
        c = np.ones(len(s), int)
        c[int(rng.integers(1, len(s) - 1))] = N - len(s) + 1
        top = np.array([(min(DS, (C - least[r]) // among[r]) - int(c[i])) // N for i, r in enumerate(s)])
        j = np.ones(len(s), int)
        while j.sum() < DN // N - 1: j[int(rng.choice(np.flatnonzero(j < top)))] += 1
        k[s, q] = N * j + c
    for r in range(N):
        n = alone[r]
        if n == 0: continue
        z = min(C - int(k[r].sum()), n * DS)
        w = least[r] + N * int(rng.integers(0, (z - least[r]) // N + 1))
        for q in range(N):
            if src[q] == [r]:
                n -= 1
                u = int(rng.integers(max(lo, w - DS * n), min(DS, w - lo * n) + 1))
                k[r, q] = u; w -= u
    e = [[] for r in range(N)]
    for q, s in enumerate(src):
        v = some(int(k[:, q].sum()), P)
        for r in s:
            i = int(k[r, q])
            e[r] += v[:i]; v = v[i:]
    m = np.zeros((N, C), int)
    for r in range(N):
        m[r, np.sort(rng.permutation(C)[:len(e[r])])] = np.array(e[r], int)
    if flip: m = m[::-1, ::-1]
    return {**floats(rng), "cnt": np.stack([table(v) for v in m])}
def setup_inputs_spread(rng):
    d = setup_inputs(rng); v = np.array(wide(rng, N, 128, 4 * C, cols=6))
    v[np.abs(v.astype(np.float32)) < 2.0 ** -30] = 0
    d["x"] = v; return d
def check_inputs(d):
    b = []
    for k in ("x", "w"):
        v = np.abs(d[k].astype(np.float32))
        if not ((v == 0) | ((v >= 2.0 ** -30) & (v <= 2.0 ** 30))).all(): b.append("the range of " + k)
    m = np.stack([entries(a) for a in d["cnt"]])
    if m.min() < 0 or m.max() > 6: return b + ["cnt"]
    if m.sum() != N * P: return b + ["the sum of all counts"]
    runs = np.repeat(np.arange(N * C), m.reshape(-1)).reshape(N, P)
    for q in range(N):
        u = np.unique(runs[q])
        k = np.bincount(np.floor_divide(u, C), minlength=N)
        if len(u) > DN: b.append("different columns in a run")
        if k.max() > DS: b.append("different columns of one rank in a run")
        if (np.abs(np.flatnonzero(k) - q) > 2).any(): b.append("a column of a rank more than two away")
    return b
def reference(x, w, cnt):
    m = np.stack([entries(a) for a in cnt])
    runs = np.repeat(np.arange(N * C), m.reshape(-1)).reshape(N, P)
    t = np.concatenate([x[r] for r in range(N)], axis=1)
    y = np.zeros((N, 128, O * P), np.float32)
    for q in range(N):
        for b in range(B):
            c = mx_ref.quantize(cols(t, runs[q, 128 * b:128 * b + 128]))
            for o in range(O):
                i = P * o + 128 * b
                y[q][:, i:i + 128] = mx_ref.matmul(mx_ref.quantize(cut(w[q], O * b + o)), c)
    return {"y": y}

@@ -1,0 +1,400 @@
+from concourse.bass import DstId, RemoteDMATransfer
+from concourse.mybir import dt, AluOpType as A, AxisListType, ActivationFunctionType as F
+
+N, C, P, DS = 8, 128, 256, 80
+BASE = {-2: 0, -1: 80, 0: 160, 1: 288, 2: 368}
+WIN = 448
+NG, ND = 784, 128
+RG = 2064
+
+f32, bf, i32, u16, u8, c4 = "float32", "bfloat16", "int32", "uint16", "uint8", "float8_e4m3fn_x4"
+SCRATCH = {}
+for _n, _w, _d in [
+    ("ct", 8, i32), ("tabf", 8, f32), ("rsum", 1, f32), ("bcs", 32, f32), ("trs", 32, f32), ("z32", 32, f32),
+    ("tot", 32, f32), ("ip", 1, i32), ("ipa", 1, i32), ("ipg", 1, i32), ("ipg2", 1, i32), ("paf", 1, f32), ("paf5", 1, f32),
+    ("pgf", 1, f32), ("it8", 8, f32), ("offc", 8, u16), ("fm", 256, f32), ("mask", 256, f32), ("rst", 256, f32),
+    ("fm8", 40, f32), ("rst8", 40, f32), ("i16", 40, f32), ("k8", 8, f32), ("ik5", 20, f32), ("ik", 20, f32),
+    ("jt", 16, f32), ("di", 40, f32), ("di8", 8, f32), ("i2048", 40, f32), ("i800", 8, f32), ("ef", 2, f32), ("id8", 8, f32), ("dm", 8, f32),
+    ("bc", 128, f32), ("nrow", 128, f32), ("erow", 128, f32), ("nz", 128, f32), ("zrow", 128, f32), ("me", 128, f32),
+    ("se", 128, f32), ("et", 9, f32), ("fl8", 8, f32), ("fl1", 8, f32), ("de", 8, f32), ("vv", 8, f32), ("vh", 4, f32), ("pkf", 4, f32),
+    ("pk", 4, u16), ("junk", 1024, f32), ("acc", 8, f32), ("cf", 8, f32), ("comp", 16, u16),
+    ("p1", 8, f32), ("p2", 8, f32), ("p3", 8, f32), ("pos8", 8, u16), ("mrk", NG + ND, bf), ("ones", 640, bf), ("grow", NG, f32),
+    ("ka", 8, f32), ("kb", 8, f32), ("kt", 2, f32), ("kt2", 2, f32), ("sg", 1, f32), ("thr", 2, u16), ("lo", 32, f32),
+    ("lf", 20, f32), ("lst", 20, u16),
+    ("l2", 20, u16), ("wi", 20, i32), ("v8", 40, i32), ("dei", 40, i32), ("fli", 40, i32), ("def_", 40, f32), ("flf", 40, f32),
+    ("pr", 8, f32), ("pa", 1, f32), ("p0", 1, f32), ("er", 40, f32), ("ee", 40, f32), ("cc", 40, f32), ("cd", 40, f32),
+    ("po", 40, f32), ("pos", 40, u16), ("mr2", RG + 640, bf), ("g", 256, f32), ("mg", 256, f32), ("sgm", 256, f32),
+    ("st", 8, f32), ("st1", 1, f32), ("sto", 2, u16), ("h", 16, f32), ("bt", 8, f32), ("jj", 8, f32), ("dj", 8, f32),
+    ("tj", 64, f32), ("a1", 16, f32), ("a2", 16, f32), ("a3", 16, f32), ("a4", 16, f32), ("fin", 16, u16),
+    ("xb", 512, bf), ("xq", 128, c4), ("xs", 128, u8), ("xc", 208, c4), ("xcs", 208, u8),
+    ("snd", 320, c4), ("snds", 320, u8), ("win", WIN, c4), ("wins", WIN, u8), ("t2", 256, c4), ("t2s", 256, u8),
+    ("wb", 2048, bf), ("wq", 512, c4), ("ws", 512, u8), ("ysb", 512, f32),
+    ("r1b", 1, f32), ("r2b", 4, u16), ("rcb", 80, c4), ("rsb", 80, u8),
+]:
+    SCRATCH[_n] = ("sbuf", [128, _w], _d)
+SCRATCH["ps"] = ("psum", [128, 2048], f32)
+SEMAPHORES = (["cl", "xl", "wl", "l2d", "own", "vs", "ss", "ts", "gs", "ls", "ls1", "m2", "dc", "dsc",
+               "r1", "r2", "rc", "rsc", "st0", "st9"] + ["m1_%d" % s for s in range(N)])
+
+
+def needs(q):
+    return list(range(q)) if q < N // 2 else list(range(q + 1, N))
+
+
+def plan(T, topo):
+    out = []
+    for r in range(N):
+        core = T.cores[r]
+        near = [q for q in (r - 1, r + 1, r - 2, r + 2) if 0 <= q < N]
+        far = [q for q in range(N) if q not in near and q != r and r in needs(q)]
+        direct = [q for q in near if topo.may_write(core, T.cores[q])]
+        hop = [q for q in near if q not in direct]
+        relays = [c for c in topo.cores_of(core) if c != core and all(topo.may_write(c, T.cores[q]) for q in hop + far)]
+        X = [c for c in relays if topo.die(c) == topo.die(core)][0]
+        Y = [c for c in relays if topo.die(c) != topo.die(core)][0]
+        out.append({"direct": direct, "hop": hop, "hop1": hop + far, "X": X, "Y": Y})
+    return out
+
+
+def mask_of(es):
+    return sum(1 << e for e in es)
+
+
+def part(es, k, n):
+    w = len(es) // n
+    return es[k * w:k * w + w]
+
+
+def sender(g, core, T, topo):
+    def send(items, rsem, lsem):
+        tr = []
+        for dst, es, o, i in items:
+            rid, pid = topo.addr(dst, core)
+            tr.append(RemoteDMATransfer(dst_ids=[DstId(rid=rid, pnc=pid)], dma_engine_mask=mask_of(es),
+                                        remote_sem=T.sem[rsem], src=i, dst=o))
+        g.remote_dma_fused(tr, local_sem=T.sem[lsem])
+        return sum(len(es) for _, es, _, _ in items)
+    return send
+
+
+def codes(v):
+    return v.bitcast(dt.uint8)
+
+
+def slot(s, q):
+    return s - max(0, q - 2)
+
+
+def relay_program(g, core, T, topo, pl, r, first):
+    me = pl[r]
+    send = sender(g, core, T, topo)
+    n = 0
+    dsts = me["hop1"] if first else me["hop"]
+    g.wait_ge(T.sem["r1" if first else "r2"], 8)
+    it = []
+    for k, q in enumerate(dsts):
+        dst = T.cores[q]
+        es = part(topo.engines(core, dst), k, len(dsts))
+        if first:
+            it.append((dst, es, T.tot[:, 4 * r:4 * r + 1], T.r1b[:]))
+        else:
+            o = 4 * slot(r, q)
+            it.append((dst, es, T.l2[:, o:o + 4], T.r2b[:]))
+    n += send(it, "m1_%d" % r if first else "m2", "ls")
+    for q in me["hop"]:
+        if (q < r) == first:
+            dst = T.cores[q]
+            b = BASE[r - q]
+            es = topo.engines(core, dst)
+            g.wait_ge(T.sem["rc"], 8)
+            n += send([(dst, es, codes(T.win[:, b:b + DS]), codes(T.rcb[:, 0:DS]))], "dc", "ls")
+            g.wait_ge(T.sem["rsc"], 8)
+            n += send([(dst, es, T.wins[:, b:b + DS], T.rsb[:, 0:DS])], "dsc", "ls")
+    g.wait_ge(T.sem["ls"], n)
+
+
+def rank_program(g, core, T, topo):
+    pl = plan(T, topo)
+    r = T.rank_of(core)
+    if r is None:
+        for k in range(N):
+            if core == pl[k]["X"]:
+                relay_program(g, core, T, topo, pl, k, True)
+            if core == pl[k]["Y"]:
+                relay_program(g, core, T, topo, pl, k, False)
+        return
+    me = pl[r]
+    send = sender(g, core, T, topo)
+    queues = {"v": g.vector, "s": g.scalar, "t": g.tensor, "g": g, "y": g.sync}
+    own = {"v": "vs", "s": "ss", "t": "ts", "g": "gs"}
+    count = {"v": 0, "s": 0, "t": 0, "g": 0}
+    ev, seen, final = {}, {}, {}
+
+    def need(q, *keys):
+        m = {}
+        for k in keys:
+            s, v = ev[k]
+            m[s] = max(m.get(s, 0), v)
+        for s, v in m.items():
+            if seen.get((q, s), 0) < v:
+                queues[q].wait_ge(T.sem[s], v)
+                seen[(q, s)] = v
+
+    def do(q, fn, reads, write, *a, **kw):
+        need(q, *reads)
+        fn(*a, **kw).then_inc(T.sem[own[q]], 1)
+        count[q] += 1
+        ev[write] = (own[q], count[q])
+
+    def dma(q, reads, write, sem, out, in_):
+        need(q, *reads)
+        queues[q].dma_start(out, in_).then_inc(T.sem[sem], 16)
+        final[sem] = final.get(sem, 0) + 16
+        ev[write] = (sem, final[sem])
+
+    V, S = g.vector, g.scalar
+
+    for k in range(4):
+        for q, j in (("y", 2 * k), ("s", 2 * k + 1)):
+            dma(q, (), "ct", "cl", T.ct[16 * j:16 * j + 16, 0:8], T.cnt[:])
+    dma("y", (), "xb", "xl", T.xb[:], T.x[:])
+
+    do("v", V.memset, (), "z32", T.z32[:], 0.0)
+    do("g", g.iota, (), "ip", T.ip[:], [[1, 1]], 0, 1)
+
+    def iota(name, pattern, base=0):
+        do("g", g.iota, (), name, T[name][:], pattern, base, 0, allow_small_or_imprecise_dtypes=True)
+    iota("it8", [[2, 4], [0, 2]])
+    iota("i16", [[16, 40]])
+    iota("fm", [[0, 16], [1, 16]])
+    do("v", V.tensor_scalar, ("ip",), "ipa", T.ipa[:], T.ip[:], 15, None, A.bitwise_and)
+    do("v", V.tensor_scalar, ("ip",), "ipg", T.ipg[:], T.ip[:], 4, 1, A.logical_shift_right, A.bitwise_and)
+    do("v", V.tensor_copy, ("ipa",), "paf", T.paf[:], T.ipa[:])
+    do("v", V.tensor_copy, ("ipg",), "pgf", T.pgf[:], T.ipg[:])
+    do("v", V.tensor_scalar, ("paf",), "paf5", T.paf5[:], T.paf[:], 0.5, None, A.add)
+    do("v", V.tensor_scalar, ("it8", "pgf"), "offc", T.offc[:], T.it8[:], T.pgf[:], None, A.add)
+    do("v", V.tensor_scalar, ("fm", "paf"), "mask", T.mask[:], T.fm[:], T.paf[:], None, A.is_equal)
+    do("v", V.tensor_scalar, ("fm",), "rst", T.rst[:], T.fm[:], 0.0, None, A.not_equal)
+    iota("ik5", [[0, 4], [16, 5]])
+    iota("i800", [[16, 8]], NG)
+    iota("i2048", [[16, 40]], RG)
+    iota("fm8", [[0, 5], [1, 8]])
+    iota("id8", [[1, 8]])
+    do("s", S.activation, ("i16", "paf5"), "k8", T.k8[:], T.i16[:, 0:8], F.Identity, bias=T.paf5[:])
+    do("s", S.activation, ("i16", "paf"), "ef", T.ef[:], T.i16[:, 0:2], F.Identity, bias=T.paf[:])
+    do("s", S.activation, ("i16", "paf"), "jt", T.jt[:], T.i16[:, 0:16], F.Identity, bias=T.paf[:])
+    do("s", S.activation, ("ik5", "paf"), "ik", T.ik[:], T.ik5[:], F.Identity, bias=T.paf[:])
+    do("s", S.activation, ("i800", "paf"), "di8", T.di8[:], T.i800[:], F.Identity, bias=T.paf[:])
+    do("s", S.activation, ("i2048", "paf"), "di", T.di[:], T.i2048[:], F.Identity, bias=T.paf[:])
+
+    mine = T.tot[:, 4 * r:4 * r + 1]
+    do("v", V.tensor_copy, ("ct",), "tabf", T.tabf[:], T.ct[:])
+    do("v", V.tensor_reduce, ("tabf",), "rsum", T.rsum[:], T.tabf[:], AxisListType.X, A.add)
+    do("v", V.tensor_scalar, ("z32", "rsum"), "bcs", T.bcs[:], T.z32[:], T.rsum[:], None, A.add)
+    do("v", V.transpose, ("bcs",), "trs", T.trs[:], T.bcs[:])
+    do("v", V.tensor_reduce, ("trs",), "tot", mine, T.trs[:, 0:16], AxisListType.X, A.add)
+
+    nls1, nls = 0, 0
+    need("g", "tot")
+    chip = topo.engines(core, me["X"])
+    nls1 += send([(me["X"], part(chip, 0, 2), T.r1b[:], mine)], "r1", "ls1")
+    dr = me["direct"]
+
+    def direct_engines(k):
+        return part(topo.engines(core, T.cores[dr[k]]), k, len(dr))
+    nls1 += send([(T.cores[q], direct_engines(k), mine, mine) for k, q in enumerate(dr)], "m1_%d" % r, "ls1")
+    ev["ls1"] = ("ls1", nls1)
+    dma("y", ("ls1",), "wb", "wl", T.wb[:], T.w[:])
+
+    do("v", V.tensor_copy, ("tabf", "offc"), "bc", T.bc[:], T.tabf[:, 0:8].indirect(T.offc[:]))
+    do("v", V.transpose, ("bc",), "nrow", T.nrow[:], T.bc[:])
+    do("v", V.tensor_scalar, ("nrow",), "nz", T.nz[:], T.nrow[:], 0.0, None, A.is_gt)
+    do("v", V.tensor_tensor_scan, ("nz",), "zrow", T.zrow[:], T.nz[:], T.nz[:], 0.0, A.add, A.max)
+    do("v", V.tensor_tensor_scan, ("nrow",), "erow", T.erow[:], T.nrow[:], T.nrow[:], 0.0, A.add, A.max)
+    for c in range(8):
+        do("s", S.activation, ("zrow", "k8"), "acc", T.junk[:, 128 * c:128 * c + 128], T.zrow[:], F.Sign,
+           bias=T.k8[:, c:c + 1], scale=-1.0, accum_out=T.acc[:, c:c + 1])
+    do("v", V.memset, (), "et0", T.et[:, 0:1], 0.0)
+    do("v", V.tensor_tensor, ("erow", "mask"), "me", T.me[:], T.erow[:], T.mask[:, 0:128], A.mult)
+    do("v", V.tensor_scalar, ("tabf",), "fl8", T.fl8[:], T.tabf[:], 0.0, 128.0, A.is_gt, A.mult)
+    do("v", V.tensor_tensor_scan, ("me", "rst"), "se", T.se[:], T.rst[:, 0:128], T.me[:], 0.0, A.mult, A.add)
+    do("v", V.tensor_copy, ("se",), "et", T.et[:, 1:9], T.se[:, 15:128:16])
+    do("v", V.tensor_tensor, ("et", "et0"), "de", T.de[:], T.et[:, 1:9], T.et[:, 0:8], A.subtract)
+    do("v", V.tensor_tensor, ("de", "fl8"), "vv", T.vv[:], T.de[:], T.fl8[:], A.add)
+    do("v", V.tensor_scalar, ("vv",), "vh", T.vh[:], T.vv[:, 1:8:2], 256.0, None, A.mult)
+    do("v", V.tensor_tensor, ("vv", "vh"), "pkf", T.pkf[:], T.vv[:, 0:8:2], T.vh[:], A.add)
+    do("v", V.tensor_copy, ("pkf",), "pk", T.pk[:], T.pkf[:])
+
+    need("g", "pk")
+    nls += send([(me["Y"], part(topo.engines(core, me["Y"]), 1, 2), T.r2b[:], T.pk[:])], "r2", "ls")
+    nls += send([(T.cores[q], direct_engines(k), T.l2[:, 4 * slot(r, q):4 * slot(r, q) + 4], T.pk[:])
+                 for k, q in enumerate(dr)], "m2", "ls")
+    o = 4 * slot(r, r)
+    dma("y", ("pk",), "l2own", "l2d", T.l2[:, o:o + 4], T.pk[:])
+
+    do("v", V.quantize_mx, ("xb",), "xq", T.xq[:], T.xs[:], T.xb[:])
+    do("v", V.memset, (), "comp0", T.comp[:, 8:16], 127)
+    do("v", V.tensor_scalar, ("acc",), "cf", T.cf[:], T.acc[:], 0.5, 64.0, A.mult, A.add)
+    do("v", V.tensor_scalar, ("cf",), "comp", T.comp[:, 0:8], T.cf[:], 127.0, None, A.min)
+    do("v", V.tensor_copy, ("xq", "comp", "comp0"), "xc", T.xc[:].bitcast(dt.uint32),
+       T.xq[:].bitcast(dt.uint32).indirect(T.comp[:, 0:13]))
+    do("s", S.activation, ("xq", "comp", "comp0"), "xcs", T.xcs[:], T.xs[:].indirect(T.comp[:, 0:13]), F.Copy)
+    dma("y", ("xc",), "own", "own", codes(T.win[:, 160:288]), codes(T.xc[:, 0:128]))
+    dma("y", ("xcs",), "own", "own", T.wins[:, 160:288], T.xcs[:, 0:128])
+
+    do("v", V.memset, (), "ones", T.ones[:], 1.0)
+    do("v", V.memset, (), "mrk0", T.mrk[:, 0:NG], 0.0)
+    do("v", V.tensor_scalar, ("tabf",), "fl1", T.fl1[:], T.tabf[:], 0.0, None, A.is_gt)
+    do("v", V.tensor_tensor, ("et", "di8"), "p1", T.p1[:], T.et[:, 1:9], T.di8[:], A.subtract)
+    do("v", V.tensor_tensor, ("p1", "fl1"), "p2", T.p2[:], T.p1[:], T.fl1[:], A.mult)
+    do("v", V.tensor_tensor, ("p2", "di8"), "p3", T.p3[:], T.p2[:], T.di8[:], A.add)
+    do("v", V.tensor_copy, ("p3",), "pos8", T.pos8[:], T.p3[:])
+    do("v", V.tensor_copy, ("pos8", "ones", "mrk0"), "mrk", T.mrk[:].indirect(T.pos8[:]), T.ones[:, 0:128])
+    do("v", V.tensor_tensor_scan, ("mrk",), "grow", T.grow[:], T.mrk[:, 0:NG], T.mrk[:, 0:NG], 0.0, A.add, A.max)
+    up = r >= N // 2
+    for k, (e, v) in enumerate(((5, 2), (10, -3), (15, 4), (20, -2))):
+        do("v", V.tensor_scalar, ("ef",), "ka", T.ka[:, 2 * k:2 * k + 2], T.ef[:], float(e), float(v * P), A.is_ge, A.mult)
+    do("v", V.tensor_tensor, ("ka",), "kb", T.kb[:, 0:4], T.ka[:, 0:4], T.ka[:, 4:8], A.add)
+    do("v", V.tensor_tensor, ("kb",), "kb2", T.kb[:, 4:6], T.kb[:, 0:2], T.kb[:, 2:4], A.add)
+    do("v", V.tensor_scalar, ("kb2",), "kt", T.kt[:], T.kb[:, 4:6], float((r - 1) * P - (N * P if up else 0)), None, A.add)
+    kt = T.kt
+    if up:
+        do("v", V.tensor_scalar, ("kt", "tot"), "kt", T.kt2[:], T.kt[:], mine, None, A.add)
+        kt = T.kt2
+    do("v", V.tensor_scalar, ("fm8",), "rst8", T.rst8[:], T.fm8[:], 0.0, None, A.not_equal)
+    do("v", V.tensor_scalar, ("id8", "paf"), "dm", T.dm[:], T.id8[:], T.paf[:], None, A.is_equal)
+    do("v", V.memset, (), "mr0", T.mr2[:, 0:256], 0.0)
+
+    for s in range(N):
+        if s == r:
+            continue
+        d = pl[s]
+        if r in d["hop1"]:
+            ev["m1_%d" % s] = ("m1_%d" % s, 8 // len(d["hop1"]))
+        elif r in d["direct"]:
+            ev["m1_%d" % s] = ("m1_%d" % s, 8 // len(d["direct"]))
+    n2, nd = 0, 0
+    for s in range(N):
+        if r in pl[s]["hop"]:
+            n2 += 8 // len(pl[s]["hop"])
+            nd += 8
+        elif r in pl[s]["direct"]:
+            n2 += 8 // len(pl[s]["direct"])
+            nd += 8 // len(pl[s]["direct"])
+    ev["m2"], ev["dc"], ev["dsc"] = ("m2", n2), ("dc", nd), ("dsc", nd)
+
+    ns = [] if r in (0, N - 1) else needs(r)
+    keys = ["m1_%d" % s for s in ns]
+    if not ns:
+        do("v", V.tensor_scalar, ("kt",), "thr", T.thr[:], kt[:], 768.0, None, A.min)
+    else:
+        sg = T.tot[:, 4 * ns[0]:4 * ns[0] + 1]
+        if len(ns) > 1:
+            do("v", V.tensor_reduce, keys, "sg", T.sg[:], T.tot[:, 4 * ns[0]:4 * ns[-1] + 1:4], AxisListType.X, A.add)
+            sg, keys = T.sg[:], ["sg"]
+        do("v", V.tensor_scalar, ["kt"] + keys, "thr", T.thr[:], kt[:], sg, 768.0, A.add if up else A.subtract, A.min)
+    do("v", V.tensor_copy, ("thr", "grow"), "lo", T.lo[:], T.grow[:].indirect(T.thr[:]))
+    do("v", V.tensor_tensor, ("lo", "ik"), "lf", T.lf[:], T.lo[:, 0:20], T.ik[:], A.add)
+    do("v", V.tensor_copy, ("lf",), "lst", T.lst[:], T.lf[:])
+    for k in (0, 1):
+        do("v", V.tensor_copy, ("lst", "xc"), "snd%d" % k, T.snd[:, 160 * k:160 * k + 160].bitcast(dt.uint32),
+           T.xc[:].bitcast(dt.uint32).indirect(T.lst[:, 10 * k:10 * k + 10]))
+        do("s", S.activation, ("lst", "xcs"), "snds%d" % k, T.snds[:, 160 * k:160 * k + 160],
+           T.xcs[:].indirect(T.lst[:, 10 * k:10 * k + 10]), F.Copy)
+    col = {r - 1: 0, r + 1: 80, r - 2: 160, r + 2: 240}
+    need("g", "snd0")
+    it, it2 = [], []
+    for q in me["hop"]:
+        dst, c = (me["X"] if q < r else me["Y"]), col[q]
+        es = part(topo.engines(core, dst), 0 if q < r else 1, 2)
+        it.append((dst, es, codes(T.rcb[:]), codes(T.snd[:, c:c + DS])))
+        it2.append((dst, es, T.rsb[:], T.snds[:, c:c + DS]))
+    nls += send(it, "rc", "ls")
+    need("g", "snds0")
+    nls += send(it2, "rsc", "ls")
+    need("g", "snd1")
+    it, it2 = [], []
+    for k, q in enumerate(dr):
+        c, b = col[q], BASE[r - q]
+        it.append((T.cores[q], direct_engines(k), codes(T.win[:, b:b + DS]), codes(T.snd[:, c:c + DS])))
+        it2.append((T.cores[q], direct_engines(k), T.wins[:, b:b + DS], T.snds[:, c:c + DS]))
+    nls += send(it, "dc", "ls")
+    need("g", "snds1")
+    nls += send(it2, "dsc", "ls")
+
+    fi, hi = max(0, r - 2), min(N - 1, r + 2)
+    n = hi - fi + 1
+    for s in range(fi, hi + 1):
+        if s != r:
+            do("v", V.memset, (), "bt", T.bt[:, s - fi:s - fi + 1], float(BASE[s - r]))
+    do("v", V.tensor_scalar, ("lo",), "bt", T.bt[:, r - fi:r - fi + 1], T.lo[:, 20:21], float(BASE[0]), None, A.add)
+    if up:
+        known = list(range(fi, N))
+        do("v", V.tensor_reduce, ["m1_%d" % s for s in known if s != r] + ["tot"], "pa", T.pa[:],
+           T.tot[:, 4 * fi:4 * (N - 1) + 1:4], AxisListType.X, A.add)
+        do("v", V.tensor_scalar, ("pa",), "pr0", T.pr[:, fi:fi + 1], T.pa[:], -1.0, float((N - r) * P), A.mult, A.add)
+        do("v", V.tensor_scan if False else V.tensor_tensor_scan, ("pr0", "z32"), "pr", T.pr[:, fi + 1:hi + 1],
+           T.tot[:, 4 * fi:4 * (hi - 1) + 1:4], T.z32[:, 0:hi - fi], T.pr[:, fi:fi + 1], A.add, A.add)
+    else:
+        do("v", V.memset, (), "pr0", T.pr[:, 0:1], float(-r * P))
+        do("v", V.tensor_tensor_scan, ["m1_%d" % s for s in range(hi) if s != r] + ["tot", "z32"], "pr", T.pr[:, 1:hi + 1],
+           T.tot[:, 0:4 * (hi - 1) + 1:4], T.z32[:, 0:hi], float(-r * P), A.add, A.add)
+    prs = T.pr[:, fi:hi + 1]
+    do("v", V.tensor_copy, ("m2", "l2own"), "wi", T.wi[:, 0:4 * n], T.l2[:, 0:4 * n])
+    do("v", V.tensor_scalar, ("wi",), "v8a", T.v8[:, 0:8 * n:2], T.wi[:, 0:4 * n], 255, None, A.bitwise_and)
+    do("v", V.tensor_scalar, ("wi",), "v8", T.v8[:, 1:8 * n:2], T.wi[:, 0:4 * n], 8, None, A.logical_shift_right)
+    do("v", V.tensor_scalar, ("v8a", "v8"), "dei", T.dei[:, 0:8 * n], T.v8[:, 0:8 * n], 127, None, A.bitwise_and)
+    do("v", V.tensor_scalar, ("v8",), "fli", T.fli[:, 0:8 * n], T.v8[:, 0:8 * n], 7, None, A.logical_shift_right)
+    do("v", V.tensor_copy, ("dei",), "def_", T.def_[:, 0:8 * n], T.dei[:, 0:8 * n])
+    do("v", V.tensor_tensor, ("def_", "pr", "pr0"), "def2", T.def_[:, 0:8 * n:8], T.dei[:, 0:8 * n:8], prs, A.add)
+    do("v", V.tensor_tensor_scan, ("def2", "rst8"), "er", T.er[:, 0:8 * n], T.rst8[:, 0:8 * n], T.def_[:, 0:8 * n], 0.0, A.mult, A.add)
+    do("v", V.tensor_tensor, ("er", "fli"), "ee", T.ee[:, 0:8 * n], T.er[:, 0:8 * n], T.fli[:, 0:8 * n], A.mult)
+    do("v", V.tensor_scalar, ("ee",), "cc", T.cc[:, 0:8 * n], T.ee[:, 0:8 * n], 1.0, None, A.is_lt)
+    do("v", V.tensor_tensor, ("cc", "di"), "cd", T.cd[:, 0:8 * n], T.cc[:, 0:8 * n], T.di[:, 0:8 * n], A.mult)
+    do("v", V.tensor_tensor, ("cd", "ee"), "po", T.po[:, 0:8 * n], T.ee[:, 0:8 * n], T.cd[:, 0:8 * n], A.max)
+    do("v", V.tensor_copy, ("po",), "pos", T.pos[:, 0:8 * n], T.po[:, 0:8 * n])
+    do("v", V.tensor_copy, ("pos", "ones", "mr0"), "mr2", T.mr2[:].indirect(T.pos[:, 0:8 * n]), T.ones[:, 0:128 * n])
+    do("v", V.tensor_tensor_scan, ("mr2",), "g", T.g[:], T.mr2[:, 0:256], T.mr2[:, 0:256], 0.0, A.add, A.max)
+    do("v", V.tensor_tensor, ("pr", "pr0", "dm"), "st", T.st[:, 0:n], prs, T.dm[:, 0:n], A.mult)
+    do("v", V.tensor_reduce, ("st",), "st1", T.st1[:], T.st[:, 0:n], AxisListType.X, A.add)
+    do("v", V.tensor_scalar, ("st1",), "sto", T.sto[:, 0:1], T.st1[:], 0.0, 255.0, A.max, A.min)
+    do("v", V.tensor_tensor, ("g", "mask"), "mg", T.mg[:], T.g[:], T.mask[:], A.mult)
+    do("v", V.tensor_copy, ("sto", "g"), "h", T.h[:], T.g[:].indirect(T.sto[:, 0:1]))
+    do("v", V.tensor_tensor_scan, ("mg", "rst"), "sgm", T.sgm[:], T.rst[:], T.mg[:], 0.0, A.mult, A.add)
+    do("v", V.tensor_tensor, ("h", "bt"), "jj", T.jj[:, 0:n], T.bt[:, 0:n], T.h[:, 0:n], A.subtract)
+    do("v", V.tensor_tensor, ("jj",), "dj", T.dj[:, 0:n - 1], T.jj[:, 1:n], T.jj[:, 0:n - 1], A.subtract)
+    for k in range(1, n):
+        do("v", V.tensor_scalar, ("dj", "jt"), "tj%d" % k, T.tj[:, 16 * k - 16:16 * k], T.jt[:],
+           T.pr[:, fi + k:fi + k + 1], T.dj[:, k - 1:k], A.is_ge, A.mult)
+    prev, pkey = T.sgm[:, 15:256:16], "sgm"
+    for k in range(1, n):
+        o = T["a%d" % k]
+        do("v", V.tensor_tensor, (pkey, "tj%d" % k), "a%d" % k, o[:], prev, T.tj[:, 16 * k - 16:16 * k], A.add)
+        prev, pkey = o[:], "a%d" % k
+    do("v", V.tensor_scalar, (pkey, "jj"), "fin", T.fin[:], prev, T.jj[:, 0:1], None, A.add)
+    do("v", V.quantize_mx, ("wb",), "wq", T.wq[:], T.ws[:], T.wb[:])
+
+    for b in (0, 1):
+        do("v", V.tensor_copy, ("dc", "own", "fin"), "t%d" % b, T.t2[:, 128 * b:128 * b + 128].bitcast(dt.uint32),
+           T.win[:].bitcast(dt.uint32).indirect(T.fin[:, 8 * b:8 * b + 8]))
+        do("s", S.activation, ("dsc", "own", "fin"), "t%ds" % b, T.t2s[:, 128 * b:128 * b + 128],
+           T.wins[:].indirect(T.fin[:, 8 * b:8 * b + 8]), F.Copy)
+    for b in (0, 1):
+        for o in (0, 1):
+            k = 2 * b + o
+            do("t", g.tensor.matmul_mx, ("wq", "t%d" % b, "t%ds" % b), "mm%d" % k, T.ps[:, 512 * k:512 * k + 128],
+               T.wq[:, 128 * k:128 * k + 128], T.ws[:, 128 * k:128 * k + 128],
+               T.t2[:, 128 * b:128 * b + 128], T.t2s[:, 128 * b:128 * b + 128], True, True)
+    for b in (0, 1):
+        do("v", V.tensor_copy, ("mm%d" % (2 * b),), "y0", T.ysb[:, 128 * b:128 * b + 128], T.ps[:, 1024 * b:1024 * b + 128])
+        do("s", S.activation, ("mm%d" % (2 * b + 1),), "y1", T.ysb[:, P + 128 * b:P + 128 * b + 128],
+           T.ps[:, 1024 * b + 512:1024 * b + 640], F.Copy)
+    dma("y", ("y0",), "st0", "st0", T.y[:, 0:P], T.ysb[:, 0:P])
+    dma("s", ("y1",), "st9", "st9", T.y[:, P:2 * P], T.ysb[:, P:2 * P])
+
+    for q, s in own.items():
+        ev["end_" + q] = (s, count[q])
+    for s, v in final.items():
+        ev["end_" + s] = (s, v)
+    ev["end_ls"] = ("ls", nls)
+    need("g", *[k for k in ev if k.startswith("end_") or k.startswith("m1_")], "ls1", "m2", "dc", "dsc")

@@ -2,43 +2,58 @@ from concourse.bass import DstId, RemoteDMATransfer
 from concourse.mybir import dt, AluOpType as A, AxisListType, ActivationFunctionType as F
 
 N, C, P, DS = 8, 128, 256, 80
-BASE = {-2: 0, -1: 80, 0: 160, 1: 288, 2: 368}
-WIN = 448
+BASE = {0: 0, -1: 128, -2: 256, 2: 336, 1: 416}
+WIN = 544
+SH = 2048
 NG, ND = 784, 128
-RG = 2064
+RG = 4112
+BIG = 1.0e6
 
 f32, bf, i32, u16, u8, c4 = "float32", "bfloat16", "int32", "uint16", "uint8", "float8_e4m3fn_x4"
 SCRATCH = {}
 for _n, _w, _d in [
-    ("ct", 8, i32), ("tabf", 8, f32), ("rsum", 1, f32), ("bcs", 32, f32), ("trs", 32, f32), ("z32", 32, f32),
-    ("tot", 32, f32), ("ip", 1, i32), ("ipa", 1, i32), ("ipg", 1, i32), ("ipg2", 1, i32), ("paf", 1, f32), ("paf5", 1, f32),
-    ("pgf", 1, f32), ("it8", 8, f32), ("offc", 8, u16), ("fm", 256, f32), ("mask", 256, f32), ("rst", 256, f32),
-    ("fm8", 40, f32), ("rst8", 40, f32), ("i16", 40, f32), ("k8", 8, f32), ("ik5", 20, f32), ("ik", 20, f32),
-    ("jt", 16, f32), ("di", 40, f32), ("di8", 8, f32), ("i2048", 40, f32), ("i800", 8, f32), ("ef", 2, f32), ("id8", 8, f32), ("dm", 8, f32),
-    ("bc", 128, f32), ("nrow", 128, f32), ("erow", 128, f32), ("nz", 128, f32), ("zrow", 128, f32), ("me", 128, f32),
+    ("one", 32, f32), ("onei", 8, i32),
+    ("ct", 8, i32), ("tabf", 40, f32), ("bcs", 40, f32), ("trs", 32, f32),
+    ("tot", 32, f32), ("it8", 8, f32), ("offc", 8, u16), ("fm", 272, f32), ("fa", 256, f32), ("dg", 256, f32),
+    ("fm8", 40, f32), ("rst8", 40, f32), ("i16", 8, f32), ("k8", 8, f32), ("ik5", 12, f32), ("ik", 12, f32),
+    ("ij", 64, f32), ("jh", 64, f32), ("di", 40, f32), ("di8", 8, f32), ("idump", 40, f32), ("i800", 8, f32), ("id8", 8, f32), ("da", 8, f32), ("dm", 8, f32),
+    ("bc", 128, f32), ("nrow", 128, f32), ("erow", 128, f32), ("nz", 128, f32), ("zrow", 128, f32),
     ("se", 128, f32), ("et", 9, f32), ("fl8", 8, f32), ("fl1", 8, f32), ("de", 8, f32), ("vv", 8, f32), ("vh", 4, f32), ("pkf", 4, f32),
-    ("pk", 4, u16), ("junk", 1024, f32), ("acc", 8, f32), ("cf", 8, f32), ("comp", 16, u16),
-    ("p1", 8, f32), ("p2", 8, f32), ("p3", 8, f32), ("pos8", 8, u16), ("mrk", NG + ND, bf), ("ones", 640, bf), ("grow", NG, f32),
-    ("ka", 8, f32), ("kb", 8, f32), ("kt", 2, f32), ("kt2", 2, f32), ("sg", 1, f32), ("thr", 2, u16), ("lo", 32, f32),
-    ("lf", 20, f32), ("lst", 20, u16),
-    ("l2", 20, u16), ("wi", 20, i32), ("v8", 40, i32), ("dei", 40, i32), ("fli", 40, i32), ("def_", 40, f32), ("flf", 40, f32),
-    ("pr", 8, f32), ("pa", 1, f32), ("p0", 1, f32), ("er", 40, f32), ("ee", 40, f32), ("cc", 40, f32), ("cd", 40, f32),
-    ("po", 40, f32), ("pos", 40, u16), ("mr2", RG + 640, bf), ("g", 256, f32), ("mg", 256, f32), ("sgm", 256, f32),
-    ("st", 8, f32), ("st1", 1, f32), ("sto", 2, u16), ("h", 16, f32), ("bt", 8, f32), ("jj", 8, f32), ("dj", 8, f32),
-    ("tj", 64, f32), ("a1", 16, f32), ("a2", 16, f32), ("a3", 16, f32), ("a4", 16, f32), ("fin", 16, u16),
-    ("xb", 512, bf), ("xq", 128, c4), ("xs", 128, u8), ("xc", 208, c4), ("xcs", 208, u8),
-    ("snd", 320, c4), ("snds", 320, u8), ("win", WIN, c4), ("wins", WIN, u8), ("t2", 256, c4), ("t2s", 256, u8),
+    ("pk", 4, u16), ("junk", 1024, f32), ("acc", 8, f32), ("cf", 8, f32), ("comp", 8, u16),
+    ("p1", 24, f32), ("pos8", 8, u16), ("mrk", NG + ND, bf), ("ones", 640, bf), ("grow", NG, f32),
+    ("thr", 2, u16), ("lo", 16, f32),
+    ("lf", 12, f32), ("lst", 12, u16), ("lsp", 6, u16),
+    ("l2", 20, u16), ("wi", 20, i32), ("dei", 40, i32), ("fli", 40, i32), ("def_", 40, f32), ("zm", 8, f32),
+    ("prx", 40, f32), ("er", 40, f32), ("cd", 40, f32),
+    ("po", 40, f32), ("pos", 40, u16), ("mr2", RG + 640, bf), ("g", 256, f32), ("sgm", 256, f32), ("mn", 16, f32),
+    ("kk", 24, f32), ("ks", 96, f32), ("kx", 96, f32), ("kj", 48, f32),
+    ("st", 8, f32), ("sto", 2, u16), ("h", 16, f32), ("bt", 8, f32), ("jj", 8, f32), ("dj", 8, f32),
+    ("sgn", 64, f32), ("stp", 64, f32), ("fmn", 80, f32), ("rn", 80, f32), ("tj", 80, f32), ("sj", 80, f32), ("fin", 16, u16),
+    ("xb", 512, bf), ("xq", 128, c4), ("xs", 128, u8), ("xc", 128, c4), ("xcs", 128, u8),
+    ("sp", 80, c4), ("sps", 80, u8), ("t2", 256, c4), ("t2s", 256, u8),
     ("wb", 2048, bf), ("wq", 512, c4), ("ws", 512, u8), ("ysb", 512, f32),
-    ("r1b", 1, f32), ("r2b", 4, u16), ("rcb", 80, c4), ("rsb", 80, u8),
+    ("r1b", 1, f32), ("r2b", 4, u16), ("rcb", 128, c4), ("rsb", 128, u8),
 ]:
     SCRATCH[_n] = ("sbuf", [128, _w], _d)
+ONE = {k: i for i, k in enumerate(["paf", "paf5", "pgf", "sg", "pa", "st1", "c0", "ca", "s1", "s2", "k1", "k2", "kt",
+                                   "a0", "a1", "a2", "b0", "b1", "b2", "lop0", "lop1", "lop2"])}
+ONEI = {k: i for i, k in enumerate(["ip", "ipa", "ipg"])}
+for _k in range(N // 2):
+    SCRATCH["win%d" % _k] = ("sbuf", [128, WIN], c4)
+    SCRATCH["wins%d" % _k] = ("sbuf", [128, WIN], u8)
+    SCRATCH["dn%d" % _k] = ("sbuf", [128, 2 * DS], c4)
+    SCRATCH["dns%d" % _k] = ("sbuf", [128, 2 * DS], u8)
 SCRATCH["ps"] = ("psum", [128, 2048], f32)
-SEMAPHORES = (["cl", "xl", "wl", "l2d", "own", "vs", "ss", "ts", "gs", "ls", "ls1", "m2", "dc", "dsc",
-               "r1", "r2", "rc", "rsc", "st0", "st9"] + ["m1_%d" % s for s in range(N)])
+SEMAPHORES = (["cl", "xl", "wl", "l2d", "own", "vs", "ss", "ts", "gs", "ls", "ls1", "m2", "dc", "dsc", "ec", "es",
+               "r1", "r2", "rc", "rsc", "st0"] + ["m1_%d" % s for s in range(N)])
 
 
 def needs(q):
     return list(range(q)) if q < N // 2 else list(range(q + 1, N))
+
+
+def holder(r):
+    return r + 1 if r < N - 1 else r - 1
 
 
 def plan(T, topo):
@@ -85,6 +100,10 @@ def slot(s, q):
     return s - max(0, q - 2)
 
 
+def window(T, q):
+    return T["win%d" % (q // 2)], T["wins%d" % (q // 2)]
+
+
 def relay_program(g, core, T, topo, pl, r, first):
     me = pl[r]
     send = sender(g, core, T, topo)
@@ -101,15 +120,17 @@ def relay_program(g, core, T, topo, pl, r, first):
             o = 4 * slot(r, q)
             it.append((dst, es, T.l2[:, o:o + 4], T.r2b[:]))
     n += send(it, "m1_%d" % r if first else "m2", "ls")
-    for q in me["hop"]:
-        if (q < r) == first:
-            dst = T.cores[q]
-            b = BASE[r - q]
-            es = topo.engines(core, dst)
-            g.wait_ge(T.sem["rc"], 8)
-            n += send([(dst, es, codes(T.win[:, b:b + DS]), codes(T.rcb[:, 0:DS]))], "dc", "ls")
-            g.wait_ge(T.sem["rsc"], 8)
-            n += send([(dst, es, T.wins[:, b:b + DS], T.rsb[:, 0:DS])], "dsc", "ls")
+    q = holder(r)
+    dst = T.cores[q]
+    es = topo.engines(core, dst)
+    b = BASE[r - q]
+    win, wins = window(T, q)
+    if first:
+        g.wait_ge(T.sem["rsc"], 16)
+        n += send([(dst, es, wins[:, b:b + C], T.rsb[:])], "es", "ls")
+    else:
+        g.wait_ge(T.sem["rc"], 16)
+        n += send([(dst, es, codes(win[:, b:b + C]), codes(T.rcb[:]))], "ec", "ls")
     g.wait_ge(T.sem["ls"], n)
 
 
@@ -153,50 +174,56 @@ def rank_program(g, core, T, topo):
         ev[write] = (sem, final[sem])
 
     V, S = g.vector, g.scalar
+    X = AxisListType.X
+    one = {k: T.one[:, i:i + 1] for k, i in ONE.items()}
+    onei = {k: T.onei[:, i:i + 1] for k, i in ONEI.items()}
+    paf = one["paf"]
+    win, wins = window(T, r)
+    dn, dns = T["dn%d" % (r // 2)], T["dns%d" % (r // 2)]
+    up = r >= N // 2
+    fi, hi = max(0, r - 2), min(N - 1, r + 2)
+    n = hi - fi + 1
+    m = 8 * n
 
     for k in range(4):
         for q, j in (("y", 2 * k), ("s", 2 * k + 1)):
             dma(q, (), "ct", "cl", T.ct[16 * j:16 * j + 16, 0:8], T.cnt[:])
     dma("y", (), "xb", "xl", T.xb[:], T.x[:])
+    dma("y", (), "wb", "wl", T.wb[:], T.w[:])
 
-    do("v", V.memset, (), "z32", T.z32[:], 0.0)
-    do("g", g.iota, (), "ip", T.ip[:], [[1, 1]], 0, 1)
+    def iota(name, pattern, base=0, out=None):
+        do("g", g.iota, (), name, T[name][:] if out is None else out, pattern, base, 0, allow_small_or_imprecise_dtypes=True)
 
-    def iota(name, pattern, base=0):
-        do("g", g.iota, (), name, T[name][:], pattern, base, 0, allow_small_or_imprecise_dtypes=True)
+    def act(reads, write, out, in_, func=F.Identity, **kw):
+        do("s", S.activation, reads, write, out, in_, func, **kw)
+    z32 = T.tabf[:, 8:40]
+    do("g", g.iota, (), "ip", onei["ip"], [[1, 1]], 0, 1)
+    iota("z32", [[0, 32]], 0, z32)
     iota("it8", [[2, 4], [0, 2]])
-    iota("i16", [[16, 40]])
-    iota("fm", [[0, 16], [1, 16]])
-    do("v", V.tensor_scalar, ("ip",), "ipa", T.ipa[:], T.ip[:], 15, None, A.bitwise_and)
-    do("v", V.tensor_scalar, ("ip",), "ipg", T.ipg[:], T.ip[:], 4, 1, A.logical_shift_right, A.bitwise_and)
-    do("v", V.tensor_copy, ("ipa",), "paf", T.paf[:], T.ipa[:])
-    do("v", V.tensor_copy, ("ipg",), "pgf", T.pgf[:], T.ipg[:])
-    do("v", V.tensor_scalar, ("paf",), "paf5", T.paf5[:], T.paf[:], 0.5, None, A.add)
-    do("v", V.tensor_scalar, ("it8", "pgf"), "offc", T.offc[:], T.it8[:], T.pgf[:], None, A.add)
-    do("v", V.tensor_scalar, ("fm", "paf"), "mask", T.mask[:], T.fm[:], T.paf[:], None, A.is_equal)
-    do("v", V.tensor_scalar, ("fm",), "rst", T.rst[:], T.fm[:], 0.0, None, A.not_equal)
-    iota("ik5", [[0, 4], [16, 5]])
-    iota("i800", [[16, 8]], NG)
-    iota("i2048", [[16, 40]], RG)
-    iota("fm8", [[0, 5], [1, 8]])
-    iota("id8", [[1, 8]])
-    do("s", S.activation, ("i16", "paf5"), "k8", T.k8[:], T.i16[:, 0:8], F.Identity, bias=T.paf5[:])
-    do("s", S.activation, ("i16", "paf"), "ef", T.ef[:], T.i16[:, 0:2], F.Identity, bias=T.paf[:])
-    do("s", S.activation, ("i16", "paf"), "jt", T.jt[:], T.i16[:, 0:16], F.Identity, bias=T.paf[:])
-    do("s", S.activation, ("ik5", "paf"), "ik", T.ik[:], T.ik5[:], F.Identity, bias=T.paf[:])
-    do("s", S.activation, ("i800", "paf"), "di8", T.di8[:], T.i800[:], F.Identity, bias=T.paf[:])
-    do("s", S.activation, ("i2048", "paf"), "di", T.di[:], T.i2048[:], F.Identity, bias=T.paf[:])
+    iota("i16", [[16, 8]])
+    iota("fm", [[0, 17], [1, 16]])
+    iota("et0", [[0, 1]], 0, T.et[:, 0:1])
+    do("v", V.memset, (), "ones", T.ones[:], 1.0)
+    do("v", V.memset, (), "mrk0", T.mrk[:, 0:NG], 0.0)
+    do("v", V.tensor_scalar, ("ip",), "ipa", onei["ipa"], onei["ip"], 15, None, A.bitwise_and)
+    do("v", V.tensor_scalar, ("ip",), "ipg", onei["ipg"], onei["ip"], 4, 1, A.logical_shift_right, A.bitwise_and)
+    do("v", V.tensor_copy, ("ipa",), "paf", paf, onei["ipa"])
+    do("v", V.tensor_copy, ("ipg",), "pgf", one["pgf"], onei["ipg"])
+    do("v", V.tensor_scalar, ("it8", "pgf"), "offc", T.offc[:], T.it8[:], one["pgf"], None, A.add)
+    act(("paf",), "paf5", one["paf5"], paf, bias=0.5)
+    act(("i16", "paf5"), "k8", T.k8[:], T.i16[:], bias=one["paf5"])
+    act(("fm", "paf"), "fa", T.fa[:], T.fm[:, 1:257], F.Abs, bias=paf, scale=-1.0)
+    act(("fa",), "dg", T.dg[:], T.fa[:], F.Relu, bias=BIG, scale=-BIG)
 
     mine = T.tot[:, 4 * r:4 * r + 1]
-    do("v", V.tensor_copy, ("ct",), "tabf", T.tabf[:], T.ct[:])
-    do("v", V.tensor_reduce, ("tabf",), "rsum", T.rsum[:], T.tabf[:], AxisListType.X, A.add)
-    do("v", V.tensor_scalar, ("z32", "rsum"), "bcs", T.bcs[:], T.z32[:], T.rsum[:], None, A.add)
-    do("v", V.transpose, ("bcs",), "trs", T.trs[:], T.bcs[:])
-    do("v", V.tensor_reduce, ("trs",), "tot", mine, T.trs[:, 0:16], AxisListType.X, A.add)
+    do("v", V.tensor_copy, ("ct",), "tabf", T.tabf[:, 0:8], T.ct[:])
+    do("v", V.tensor_tensor_scan, ("tabf", "z32"), "bcs", T.bcs[:], T.tabf[:], T.tabf[:], 0.0, A.add, A.max)
+    do("v", V.transpose, ("bcs",), "trs", T.trs[:], T.bcs[:, 8:40])
+    do("v", V.tensor_reduce, ("trs",), "tot", mine, T.trs[:, 0:16], X, A.add)
 
     nls1, nls = 0, 0
     need("g", "tot")
-    chip = topo.engines(core, me["X"])
+    chip, chipy = topo.engines(core, me["X"]), topo.engines(core, me["Y"])
     nls1 += send([(me["X"], part(chip, 0, 2), T.r1b[:], mine)], "r1", "ls1")
     dr = me["direct"]
 
@@ -204,21 +231,20 @@ def rank_program(g, core, T, topo):
         return part(topo.engines(core, T.cores[dr[k]]), k, len(dr))
     nls1 += send([(T.cores[q], direct_engines(k), mine, mine) for k, q in enumerate(dr)], "m1_%d" % r, "ls1")
     ev["ls1"] = ("ls1", nls1)
-    dma("y", ("ls1",), "wb", "wl", T.wb[:], T.w[:])
 
     do("v", V.tensor_copy, ("tabf", "offc"), "bc", T.bc[:], T.tabf[:, 0:8].indirect(T.offc[:]))
     do("v", V.transpose, ("bc",), "nrow", T.nrow[:], T.bc[:])
-    do("v", V.tensor_scalar, ("nrow",), "nz", T.nz[:], T.nrow[:], 0.0, None, A.is_gt)
-    do("v", V.tensor_tensor_scan, ("nz",), "zrow", T.zrow[:], T.nz[:], T.nz[:], 0.0, A.add, A.max)
+    act(("nrow",), "nz", T.nz[:], T.nrow[:], F.Sign)
+    act(("tabf",), "fl1", T.fl1[:], T.tabf[:, 0:8], F.Sign)
+    act(("fl1",), "fl8", T.fl8[:], T.fl1[:], F.Copy, scale=128.0)
     do("v", V.tensor_tensor_scan, ("nrow",), "erow", T.erow[:], T.nrow[:], T.nrow[:], 0.0, A.add, A.max)
+    do("v", V.tensor_tensor_scan, ("nz",), "zrow", T.zrow[:], T.nz[:], T.nz[:], 0.0, A.add, A.max)
     for c in range(8):
-        do("s", S.activation, ("zrow", "k8"), "acc", T.junk[:, 128 * c:128 * c + 128], T.zrow[:], F.Sign,
-           bias=T.k8[:, c:c + 1], scale=-1.0, accum_out=T.acc[:, c:c + 1])
-    do("v", V.memset, (), "et0", T.et[:, 0:1], 0.0)
-    do("v", V.tensor_tensor, ("erow", "mask"), "me", T.me[:], T.erow[:], T.mask[:, 0:128], A.mult)
-    do("v", V.tensor_scalar, ("tabf",), "fl8", T.fl8[:], T.tabf[:], 0.0, 128.0, A.is_gt, A.mult)
-    do("v", V.tensor_tensor_scan, ("me", "rst"), "se", T.se[:], T.rst[:, 0:128], T.me[:], 0.0, A.mult, A.add)
-    do("v", V.tensor_copy, ("se",), "et", T.et[:, 1:9], T.se[:, 15:128:16])
+        act(("zrow", "k8"), "acc", T.junk[:, 128 * c:128 * c + 128], T.zrow[:], F.Sign,
+            bias=T.k8[:, c:c + 1], scale=-1.0, accum_out=T.acc[:, c:c + 1])
+    act(("acc",), "cf", T.cf[:], T.acc[:], bias=64.0, scale=0.5)
+    do("v", V.tensor_tensor_scan, ("erow", "dg"), "se", T.se[:], T.erow[:], T.dg[:, 0:128], BIG, A.min, A.max)
+    do("v", V.tensor_tensor, ("se",), "et", T.et[:, 1:9], T.se[:, 14:128:16], T.se[:, 15:128:16], A.min)
     do("v", V.tensor_tensor, ("et", "et0"), "de", T.de[:], T.et[:, 1:9], T.et[:, 0:8], A.subtract)
     do("v", V.tensor_tensor, ("de", "fl8"), "vv", T.vv[:], T.de[:], T.fl8[:], A.add)
     do("v", V.tensor_scalar, ("vv",), "vh", T.vh[:], T.vv[:, 1:8:2], 256.0, None, A.mult)
@@ -226,159 +252,185 @@ def rank_program(g, core, T, topo):
     do("v", V.tensor_copy, ("pkf",), "pk", T.pk[:], T.pkf[:])
 
     need("g", "pk")
-    nls += send([(me["Y"], part(topo.engines(core, me["Y"]), 1, 2), T.r2b[:], T.pk[:])], "r2", "ls")
-    nls += send([(T.cores[q], direct_engines(k), T.l2[:, 4 * slot(r, q):4 * slot(r, q) + 4], T.pk[:])
-                 for k, q in enumerate(dr)], "m2", "ls")
+    nls += send([(me["Y"], part(chipy, 1, 2), T.r2b[:], T.pk[:])], "r2", "ls")
     o = 4 * slot(r, r)
     dma("y", ("pk",), "l2own", "l2d", T.l2[:, o:o + 4], T.pk[:])
 
     do("v", V.quantize_mx, ("xb",), "xq", T.xq[:], T.xs[:], T.xb[:])
-    do("v", V.memset, (), "comp0", T.comp[:, 8:16], 127)
-    do("v", V.tensor_scalar, ("acc",), "cf", T.cf[:], T.acc[:], 0.5, 64.0, A.mult, A.add)
-    do("v", V.tensor_scalar, ("cf",), "comp", T.comp[:, 0:8], T.cf[:], 127.0, None, A.min)
-    do("v", V.tensor_copy, ("xq", "comp", "comp0"), "xc", T.xc[:].bitcast(dt.uint32),
-       T.xq[:].bitcast(dt.uint32).indirect(T.comp[:, 0:13]))
-    do("s", S.activation, ("xq", "comp", "comp0"), "xcs", T.xcs[:], T.xs[:].indirect(T.comp[:, 0:13]), F.Copy)
-    dma("y", ("xc",), "own", "own", codes(T.win[:, 160:288]), codes(T.xc[:, 0:128]))
-    dma("y", ("xcs",), "own", "own", T.wins[:, 160:288], T.xcs[:, 0:128])
+    do("v", V.tensor_scalar, ("cf",), "comp", T.comp[:], T.cf[:], 127.0, None, A.min)
+    do("v", V.tensor_copy, ("xq", "comp"), "xc", T.xc[:].bitcast(dt.uint32), T.xq[:].bitcast(dt.uint32).indirect(T.comp[:, 0:8]))
+    act(("xq", "comp"), "xcs", T.xcs[:], T.xs[:].indirect(T.comp[:, 0:8]), F.Copy)
+    need("g", "xc")
+    nls += send([(me["Y"], chipy, codes(T.rcb[:]), codes(T.xc[:]))], "rc", "ls")
+    need("g", "xcs")
+    nls += send([(me["X"], chip, T.rsb[:], T.xcs[:])], "rsc", "ls")
+    nls += send([(T.cores[q], direct_engines(k), T.l2[:, 4 * slot(r, q):4 * slot(r, q) + 4], T.pk[:])
+                 for k, q in enumerate(dr)], "m2", "ls")
+    dma("y", ("xc",), "own", "own", codes(win[:, 0:C]), codes(T.xc[:]))
+    dma("y", ("xcs",), "own", "own", wins[:, 0:C], T.xcs[:])
 
-    do("v", V.memset, (), "ones", T.ones[:], 1.0)
-    do("v", V.memset, (), "mrk0", T.mrk[:, 0:NG], 0.0)
-    do("v", V.tensor_scalar, ("tabf",), "fl1", T.fl1[:], T.tabf[:], 0.0, None, A.is_gt)
-    do("v", V.tensor_tensor, ("et", "di8"), "p1", T.p1[:], T.et[:, 1:9], T.di8[:], A.subtract)
-    do("v", V.tensor_tensor, ("p1", "fl1"), "p2", T.p2[:], T.p1[:], T.fl1[:], A.mult)
-    do("v", V.tensor_tensor, ("p2", "di8"), "p3", T.p3[:], T.p2[:], T.di8[:], A.add)
-    do("v", V.tensor_copy, ("p3",), "pos8", T.pos8[:], T.p3[:])
+    iota("i800", [[16, 8]], NG)
+    iota("ik5", [[0, 2], [16, 6]])
+    iota("idump", [[16, 40]], RG)
+    iota("prz", [[0, 40]], -16, T.prx[:])
+    iota("zm", [[0, 8]], -128)
+    iota("fm8", [[0, 5], [1, 8]])
+    iota("id8", [[1, 8]])
+    iota("mr0", [[0, P]], 0, T.mr2[:, SH:SH + P])
+    for s in range(fi, hi + 1):
+        if s != r and holder(s) != r:
+            iota("bt", [[0, 1]], BASE[s - r], T.bt[:, s - fi:s - fi + 1])
+    iota("ij", [[-128, n - 1], [16, 16]], SH - RG - 128, T.ij[:, 0:16 * n - 16])
+    iota("fmn", [[0, 16], [1, n]], 0, T.fmn[:, 0:16 * n])
+    act(("i800", "paf"), "di8", T.di8[:], T.i800[:], bias=paf)
+    act(("ik5", "paf"), "ik", T.ik[:], T.ik5[:], bias=paf)
+    act(("paf",), "c55", one["a0"], paf, bias=-5.5)
+    act(("paf",), "c11", one["a1"], paf, bias=-11.5)
+    act(("c55",), "s1", one["s1"], one["a0"], F.Sign)
+    act(("c11",), "s2", one["s2"], one["a1"], F.Sign)
+    act(("s1",), "k1", one["k1"], one["s1"], scale=float(-2 * P), bias=float((r + 1) * P - (N * P if up else 0)))
+    act(("s2", "k1"), "kt", one["k2"], one["s2"], scale=float(P), bias=one["k1"])
+    kt = one["k2"]
+    if up:
+        kt = one["kt"]
+        act(("kt", "tot"), "kt", kt, one["k2"], bias=mine)
+    act(("idump", "paf"), "di", T.di[:], T.idump[:], bias=paf)
+    start = float(SH - RG + ((N - r) * P if up else -r * P))
+    act(("prz", "paf"), "pr0", T.prx[:, 0:1] if r < 3 else one["c0"], paf, scale=-1.0, bias=start)
+    act(("paf",), "ca", one["ca"], paf, scale=129.0, bias=float(RG - SH))
+    act(("fm8",), "rst8", T.rst8[:], T.fm8[:], F.Sign)
+    act(("id8", "paf"), "da", T.da[:], T.id8[:], F.Abs, bias=paf, scale=-1.0)
+    act(("da",), "dm", T.dm[:], T.da[:], F.Relu, bias=1.0, scale=-1.0)
+    act(("ij",), "jh", T.jh[:, 0:16 * n - 16], T.ij[:, 0:16 * n - 16], bias=0.5)
+    act(("fmn",), "rn", T.rn[:, 0:16 * n], T.fmn[:, 0:16 * n], F.Sign)
+
+    do("v", V.tensor_tensor, ("et", "di8"), "p1", T.p1[:, 0:8], T.et[:, 1:9], T.di8[:], A.subtract)
+    do("v", V.tensor_tensor, ("p1", "fl1"), "p2", T.p1[:, 8:16], T.p1[:, 0:8], T.fl1[:], A.mult)
+    do("v", V.tensor_tensor, ("p2", "di8"), "p3", T.p1[:, 16:24], T.p1[:, 8:16], T.di8[:], A.add)
+    do("v", V.tensor_copy, ("p3",), "pos8", T.pos8[:], T.p1[:, 16:24])
     do("v", V.tensor_copy, ("pos8", "ones", "mrk0"), "mrk", T.mrk[:].indirect(T.pos8[:]), T.ones[:, 0:128])
     do("v", V.tensor_tensor_scan, ("mrk",), "grow", T.grow[:], T.mrk[:, 0:NG], T.mrk[:, 0:NG], 0.0, A.add, A.max)
-    up = r >= N // 2
-    for k, (e, v) in enumerate(((5, 2), (10, -3), (15, 4), (20, -2))):
-        do("v", V.tensor_scalar, ("ef",), "ka", T.ka[:, 2 * k:2 * k + 2], T.ef[:], float(e), float(v * P), A.is_ge, A.mult)
-    do("v", V.tensor_tensor, ("ka",), "kb", T.kb[:, 0:4], T.ka[:, 0:4], T.ka[:, 4:8], A.add)
-    do("v", V.tensor_tensor, ("kb",), "kb2", T.kb[:, 4:6], T.kb[:, 0:2], T.kb[:, 2:4], A.add)
-    do("v", V.tensor_scalar, ("kb2",), "kt", T.kt[:], T.kb[:, 4:6], float((r - 1) * P - (N * P if up else 0)), None, A.add)
-    kt = T.kt
-    if up:
-        do("v", V.tensor_scalar, ("kt", "tot"), "kt", T.kt2[:], T.kt[:], mine, None, A.add)
-        kt = T.kt2
-    do("v", V.tensor_scalar, ("fm8",), "rst8", T.rst8[:], T.fm8[:], 0.0, None, A.not_equal)
-    do("v", V.tensor_scalar, ("id8", "paf"), "dm", T.dm[:], T.id8[:], T.paf[:], None, A.is_equal)
-    do("v", V.memset, (), "mr0", T.mr2[:, 0:256], 0.0)
+    do("v", V.quantize_mx, ("wb",), "wq", T.wq[:], T.ws[:], T.wb[:])
 
     for s in range(N):
-        if s == r:
-            continue
-        d = pl[s]
-        if r in d["hop1"]:
-            ev["m1_%d" % s] = ("m1_%d" % s, 8 // len(d["hop1"]))
-        elif r in d["direct"]:
-            ev["m1_%d" % s] = ("m1_%d" % s, 8 // len(d["direct"]))
-    n2, nd = 0, 0
+        for kind in ("hop1", "direct"):
+            if r in pl[s][kind]:
+                ev["m1_%d" % s] = ("m1_%d" % s, 8 // len(pl[s][kind]))
+    n2, nd, ne = 0, 0, 0
     for s in range(N):
         if r in pl[s]["hop"]:
             n2 += 8 // len(pl[s]["hop"])
-            nd += 8
         elif r in pl[s]["direct"]:
             n2 += 8 // len(pl[s]["direct"])
-            nd += 8 // len(pl[s]["direct"])
+            nd += 8
+        if holder(s) == r:
+            ne += 8
     ev["m2"], ev["dc"], ev["dsc"] = ("m2", n2), ("dc", nd), ("dsc", nd)
+    early, earlys = (), ()
+    if ne:
+        ev["ec"], ev["es"] = ("ec", ne), ("es", ne)
+        early, earlys = ("ec",), ("es",)
+    held = [s for s in range(N) if holder(s) == r]
 
     ns = [] if r in (0, N - 1) else needs(r)
     keys = ["m1_%d" % s for s in ns]
     if not ns:
-        do("v", V.tensor_scalar, ("kt",), "thr", T.thr[:], kt[:], 768.0, None, A.min)
+        do("v", V.tensor_scalar, ("kt",), "thr", T.thr[:, 0:1], kt, 768.0, None, A.min)
     else:
         sg = T.tot[:, 4 * ns[0]:4 * ns[0] + 1]
         if len(ns) > 1:
-            do("v", V.tensor_reduce, keys, "sg", T.sg[:], T.tot[:, 4 * ns[0]:4 * ns[-1] + 1:4], AxisListType.X, A.add)
-            sg, keys = T.sg[:], ["sg"]
-        do("v", V.tensor_scalar, ["kt"] + keys, "thr", T.thr[:], kt[:], sg, 768.0, A.add if up else A.subtract, A.min)
-    do("v", V.tensor_copy, ("thr", "grow"), "lo", T.lo[:], T.grow[:].indirect(T.thr[:]))
-    do("v", V.tensor_tensor, ("lo", "ik"), "lf", T.lf[:], T.lo[:, 0:20], T.ik[:], A.add)
-    do("v", V.tensor_copy, ("lf",), "lst", T.lst[:], T.lf[:])
-    for k in (0, 1):
-        do("v", V.tensor_copy, ("lst", "xc"), "snd%d" % k, T.snd[:, 160 * k:160 * k + 160].bitcast(dt.uint32),
-           T.xc[:].bitcast(dt.uint32).indirect(T.lst[:, 10 * k:10 * k + 10]))
-        do("s", S.activation, ("lst", "xcs"), "snds%d" % k, T.snds[:, 160 * k:160 * k + 160],
-           T.xcs[:].indirect(T.lst[:, 10 * k:10 * k + 10]), F.Copy)
-    col = {r - 1: 0, r + 1: 80, r - 2: 160, r + 2: 240}
-    need("g", "snd0")
-    it, it2 = [], []
-    for q in me["hop"]:
-        dst, c = (me["X"] if q < r else me["Y"]), col[q]
-        es = part(topo.engines(core, dst), 0 if q < r else 1, 2)
-        it.append((dst, es, codes(T.rcb[:]), codes(T.snd[:, c:c + DS])))
-        it2.append((dst, es, T.rsb[:], T.snds[:, c:c + DS]))
-    nls += send(it, "rc", "ls")
-    need("g", "snds0")
-    nls += send(it2, "rsc", "ls")
-    need("g", "snd1")
-    it, it2 = [], []
-    for k, q in enumerate(dr):
-        c, b = col[q], BASE[r - q]
-        it.append((T.cores[q], direct_engines(k), codes(T.win[:, b:b + DS]), codes(T.snd[:, c:c + DS])))
-        it2.append((T.cores[q], direct_engines(k), T.wins[:, b:b + DS], T.snds[:, c:c + DS]))
-    nls += send(it, "dc", "ls")
-    need("g", "snds1")
-    nls += send(it2, "dsc", "ls")
+            do("v", V.tensor_reduce, keys, "sg", one["sg"], T.tot[:, 4 * ns[0]:4 * ns[-1] + 1:4], X, A.add)
+            sg, keys = one["sg"], ["sg"]
+        do("v", V.tensor_scalar, ["kt"] + keys, "thr", T.thr[:, 0:1], kt, sg, 768.0, A.add if up else A.subtract, A.min)
+    do("v", V.tensor_copy, ("thr", "grow"), "lo", T.lo[:], T.grow[:].indirect(T.thr[:, 0:1]))
+    do("v", V.tensor_tensor, ("lo", "ik"), "lf", T.lf[:], T.lo[:, 0:12], T.ik[:], A.add)
+    do("v", V.tensor_scalar, ("lf",), "lst", T.lst[:], T.lf[:], 127.0, None, A.min)
 
-    fi, hi = max(0, r - 2), min(N - 1, r + 2)
-    n = hi - fi + 1
-    for s in range(fi, hi + 1):
-        if s != r:
-            do("v", V.memset, (), "bt", T.bt[:, s - fi:s - fi + 1], float(BASE[s - r]))
-    do("v", V.tensor_scalar, ("lo",), "bt", T.bt[:, r - fi:r - fi + 1], T.lo[:, 20:21], float(BASE[0]), None, A.add)
-    if up:
-        known = list(range(fi, N))
-        do("v", V.tensor_reduce, ["m1_%d" % s for s in known if s != r] + ["tot"], "pa", T.pa[:],
-           T.tot[:, 4 * fi:4 * (N - 1) + 1:4], AxisListType.X, A.add)
-        do("v", V.tensor_scalar, ("pa",), "pr0", T.pr[:, fi:fi + 1], T.pa[:], -1.0, float((N - r) * P), A.mult, A.add)
-        do("v", V.tensor_scan if False else V.tensor_tensor_scan, ("pr0", "z32"), "pr", T.pr[:, fi + 1:hi + 1],
-           T.tot[:, 4 * fi:4 * (hi - 1) + 1:4], T.z32[:, 0:hi - fi], T.pr[:, fi:fi + 1], A.add, A.add)
-    else:
-        do("v", V.memset, (), "pr0", T.pr[:, 0:1], float(-r * P))
-        do("v", V.tensor_tensor_scan, ["m1_%d" % s for s in range(hi) if s != r] + ["tot", "z32"], "pr", T.pr[:, 1:hi + 1],
-           T.tot[:, 0:4 * (hi - 1) + 1:4], T.z32[:, 0:hi], float(-r * P), A.add, A.add)
-    prs = T.pr[:, fi:hi + 1]
+    def pick(name, dst, dsts, list_, lkey, src, srcs, keys, skeys):
+        do("v", V.tensor_copy, (lkey,) + keys, name, dst.bitcast(dt.uint32), src.bitcast(dt.uint32).indirect(list_))
+        act((lkey,) + skeys, name + "s", dsts, srcs.indirect(list_), F.Copy)
+
+    def late(q, src, srcs, w, kc, ks):
+        b = BASE[r - q]
+        to, tos = window(T, q)
+        es = topo.engines(core, T.cores[q])
+        need("g", *kc)
+        a = send([(T.cores[q], es, codes(to[:, b:b + w]), codes(src[:, 0:w]))], "dc", "ls")
+        need("g", *ks)
+        return a + send([(T.cores[q], es, tos[:, b:b + w], srcs[:, 0:w])], "dsc", "ls")
+    if r + 2 < N:
+        pick("snd0", T.sp[:, 0:DS], T.sps[:, 0:DS], T.lst[:, 0:5], "lst", T.xc[:, 0:C], T.xcs[:, 0:C], ("xc",), ("xcs",))
+        nls += late(r + 2, T.sp, T.sps, DS, ("snd0",), ("snd0s",))
+    if r >= 2:
+        pick("snd1", dn[:, 0:DS], dns[:, 0:DS], T.lst[:, 6:11], "lst", T.xc[:, 0:C], T.xcs[:, 0:C], ("xc",), ("xcs",))
+    act(("lo",), "bts", T.bt[:, r - fi:r - fi + 1], T.lo[:, 12:13], F.Copy, bias=float(BASE[0]))
+
+    if r == 3:
+        do("v", V.tensor_scalar, ("prz", "pr0", "m1_0"), "pr0", T.prx[:, 0:1], T.tot[:, 0:1], one["c0"], None, A.add)
+    elif up:
+        do("v", V.tensor_reduce, ["m1_%d" % s for s in range(fi, N) if s != r] + ["tot"], "pa", one["pa"],
+           T.tot[:, 4 * fi:4 * (N - 1) + 1:4], X, A.add)
+        do("v", V.tensor_scalar, ("prz", "pr0", "pa"), "pr0", T.prx[:, 0:1], one["pa"], -1.0, one["c0"], A.mult, A.add)
+    do("v", V.tensor_tensor_scan, ["m1_%d" % s for s in range(fi, hi) if s != r] + ["tot", "zm", "pr0", "prz"], "prx",
+       T.prx[:, 8:8 * (n - 1) + 1:8], T.tot[:, 4 * fi:4 * (hi - 1) + 1:4], T.zm[:, 0:n - 1], T.prx[:, 0:1], A.add, A.add)
+    for k in range(1, n):
+        act(("prx", "jh"), "sgn", T.sgn[:, 16 * k - 16:16 * k], T.jh[:, 16 * k - 16:16 * k], F.Sign,
+            bias=T.prx[:, 8 * k:8 * k + 1], scale=-1.0)
+    act(("sgn",), "stp", T.stp[:, 0:16 * n - 16], T.sgn[:, 0:16 * n - 16], F.Relu, scale=-1.0)
     do("v", V.tensor_copy, ("m2", "l2own"), "wi", T.wi[:, 0:4 * n], T.l2[:, 0:4 * n])
-    do("v", V.tensor_scalar, ("wi",), "v8a", T.v8[:, 0:8 * n:2], T.wi[:, 0:4 * n], 255, None, A.bitwise_and)
-    do("v", V.tensor_scalar, ("wi",), "v8", T.v8[:, 1:8 * n:2], T.wi[:, 0:4 * n], 8, None, A.logical_shift_right)
-    do("v", V.tensor_scalar, ("v8a", "v8"), "dei", T.dei[:, 0:8 * n], T.v8[:, 0:8 * n], 127, None, A.bitwise_and)
-    do("v", V.tensor_scalar, ("v8",), "fli", T.fli[:, 0:8 * n], T.v8[:, 0:8 * n], 7, None, A.logical_shift_right)
-    do("v", V.tensor_copy, ("dei",), "def_", T.def_[:, 0:8 * n], T.dei[:, 0:8 * n])
-    do("v", V.tensor_tensor, ("def_", "pr", "pr0"), "def2", T.def_[:, 0:8 * n:8], T.dei[:, 0:8 * n:8], prs, A.add)
-    do("v", V.tensor_tensor_scan, ("def2", "rst8"), "er", T.er[:, 0:8 * n], T.rst8[:, 0:8 * n], T.def_[:, 0:8 * n], 0.0, A.mult, A.add)
-    do("v", V.tensor_tensor, ("er", "fli"), "ee", T.ee[:, 0:8 * n], T.er[:, 0:8 * n], T.fli[:, 0:8 * n], A.mult)
-    do("v", V.tensor_scalar, ("ee",), "cc", T.cc[:, 0:8 * n], T.ee[:, 0:8 * n], 1.0, None, A.is_lt)
-    do("v", V.tensor_tensor, ("cc", "di"), "cd", T.cd[:, 0:8 * n], T.cc[:, 0:8 * n], T.di[:, 0:8 * n], A.mult)
-    do("v", V.tensor_tensor, ("cd", "ee"), "po", T.po[:, 0:8 * n], T.ee[:, 0:8 * n], T.cd[:, 0:8 * n], A.max)
-    do("v", V.tensor_copy, ("po",), "pos", T.pos[:, 0:8 * n], T.po[:, 0:8 * n])
-    do("v", V.tensor_copy, ("pos", "ones", "mr0"), "mr2", T.mr2[:].indirect(T.pos[:, 0:8 * n]), T.ones[:, 0:128 * n])
-    do("v", V.tensor_tensor_scan, ("mr2",), "g", T.g[:], T.mr2[:, 0:256], T.mr2[:, 0:256], 0.0, A.add, A.max)
-    do("v", V.tensor_tensor, ("pr", "pr0", "dm"), "st", T.st[:, 0:n], prs, T.dm[:, 0:n], A.mult)
-    do("v", V.tensor_reduce, ("st",), "st1", T.st1[:], T.st[:, 0:n], AxisListType.X, A.add)
-    do("v", V.tensor_scalar, ("st1",), "sto", T.sto[:, 0:1], T.st1[:], 0.0, 255.0, A.max, A.min)
-    do("v", V.tensor_tensor, ("g", "mask"), "mg", T.mg[:], T.g[:], T.mask[:], A.mult)
+    wi = T.wi[:, 0:4 * n]
+    do("v", V.tensor_scalar, ("wi",), "dei", T.dei[:, 0:m:2], wi, 127, None, A.bitwise_and)
+    do("v", V.tensor_scalar, ("wi",), "dei2", T.dei[:, 1:m:2], wi, 8, 127, A.logical_shift_right, A.bitwise_and)
+    do("v", V.tensor_scalar, ("wi",), "fli", T.fli[:, 0:m:2], wi, 7, 1, A.logical_shift_right, A.bitwise_and)
+    do("v", V.tensor_scalar, ("wi",), "fli2", T.fli[:, 1:m:2], wi, 15, None, A.logical_shift_right)
+    do("v", V.tensor_tensor, ("dei2", "prx"), "def_", T.def_[:, 0:m], T.dei[:, 0:m], T.prx[:, 0:m], A.add)
+    do("v", V.tensor_tensor_scan, ("def_", "rst8"), "er", T.er[:, 0:m], T.rst8[:, 0:m], T.def_[:, 0:m], 0.0, A.mult, A.add)
+    do("v", V.tensor_tensor, ("er", "fli2"), "cd", T.cd[:, 0:m], T.er[:, 0:m], T.fli[:, 0:m], A.mult)
+    do("v", V.tensor_tensor, ("cd", "di"), "po", T.po[:, 0:m], T.cd[:, 0:m], T.di[:, 0:m], A.add)
+
+    jobs = [(r - 1, r - 2)] if r >= 2 else []
+    jobs += [(s, r) for s in held]
+    for k, (s, q) in enumerate(jobs):
+        b = 8 * slot(s, r)
+        act(("po", "ca"), "pq%d" % k, T.kj[:, 8 * k:8 * k + 8], T.po[:, b:b + 8], scale=-1.0, bias=float(SH + (q - r) * P) + 0.5)
+        act(("pq%d" % k,), "a%d" % k, T.kk[:, 8 * k:8 * k + 8], T.kj[:, 8 * k:8 * k + 8], F.Sign, accum_out=one["a%d" % k])
+        act(("a%d" % k,), "b%d" % k, one["b%d" % k], one["a%d" % k], scale=0.5, bias=4.0)
+        act(("b%d" % k, "z32"), "ks%d" % k, T.ks[:, 32 * k:32 * k + 32], z32, bias=one["b%d" % k])
+    do("v", V.tensor_copy, ("po",), "pos", T.pos[:, 0:m], T.po[:, 0:m])
+    do("v", V.tensor_tensor, ("prx", "dm"), "st", T.st[:, 0:n], T.prx[:, 0:m:8], T.dm[:, 0:n], A.mult)
+    do("v", V.tensor_reduce, ("st",), "st1", one["st1"], T.st[:, 0:n], X, A.add)
+    do("v", V.tensor_scalar, ("st1", "ca"), "sto", T.sto[:, 0:1], one["st1"], one["ca"], 255.0, A.add, A.min)
+    if r >= 2:
+        do("v", V.transpose, ("ks0",), "kx0", T.kx[:, 0:32], T.ks[:, 0:32])
+        do("v", V.tensor_reduce, ("kx0",), "lop0", one["lop0"], T.kx[:, 0:16], X, A.add)
+        do("v", V.tensor_scalar, ("lop0", "ik"), "lsp", T.lsp[:, 0:5], T.ik[:, 0:5], one["lop0"], 127.0, A.add, A.min)
+        b = BASE[-1]
+        pick("snd2", dn[:, DS:2 * DS], dns[:, DS:2 * DS], T.lsp[:, 0:5], "lsp", win[:, b:b + C], wins[:, b:b + C], early, earlys)
+        nls += late(r - 2, dn, dns, 2 * DS, ("snd1", "snd2"), ("snd1s", "snd2s"))
+    for k, (s, q) in enumerate(jobs):
+        if q == r:
+            do("v", V.transpose, ("ks%d" % k,), "kx%d" % k, T.kx[:, 32 * k:32 * k + 32], T.ks[:, 32 * k:32 * k + 32])
+            act(("kx%d" % k,), "lop%d" % k, T.junk[:, 16 * k:16 * k + 16], T.kx[:, 32 * k:32 * k + 16], F.Copy, accum_out=one["lop%d" % k])
+            act(("lop%d" % k,), "bts", T.bt[:, s - fi:s - fi + 1], one["lop%d" % k], F.Copy, bias=float(BASE[s - r]))
+
+    do("v", V.tensor_copy, ("pos", "ones", "mr0"), "mr2", T.mr2[:].indirect(T.pos[:, 0:m]), T.ones[:, 0:16 * m])
+    do("v", V.tensor_tensor_scan, ("mr2",), "g", T.g[:], T.mr2[:, SH:SH + P], T.mr2[:, SH:SH + P], 0.0, A.add, A.max)
     do("v", V.tensor_copy, ("sto", "g"), "h", T.h[:], T.g[:].indirect(T.sto[:, 0:1]))
-    do("v", V.tensor_tensor_scan, ("mg", "rst"), "sgm", T.sgm[:], T.rst[:], T.mg[:], 0.0, A.mult, A.add)
-    do("v", V.tensor_tensor, ("h", "bt"), "jj", T.jj[:, 0:n], T.bt[:, 0:n], T.h[:, 0:n], A.subtract)
+    do("v", V.tensor_tensor, ("h", "bt", "bts"), "jj", T.jj[:, 0:n], T.bt[:, 0:n], T.h[:, 0:n], A.subtract)
     do("v", V.tensor_tensor, ("jj",), "dj", T.dj[:, 0:n - 1], T.jj[:, 1:n], T.jj[:, 0:n - 1], A.subtract)
     for k in range(1, n):
-        do("v", V.tensor_scalar, ("dj", "jt"), "tj%d" % k, T.tj[:, 16 * k - 16:16 * k], T.jt[:],
-           T.pr[:, fi + k:fi + k + 1], T.dj[:, k - 1:k], A.is_ge, A.mult)
-    prev, pkey = T.sgm[:, 15:256:16], "sgm"
-    for k in range(1, n):
-        o = T["a%d" % k]
-        do("v", V.tensor_tensor, (pkey, "tj%d" % k), "a%d" % k, o[:], prev, T.tj[:, 16 * k - 16:16 * k], A.add)
-        prev, pkey = o[:], "a%d" % k
-    do("v", V.tensor_scalar, (pkey, "jj"), "fin", T.fin[:], prev, T.jj[:, 0:1], None, A.add)
-    do("v", V.quantize_mx, ("wb",), "wq", T.wq[:], T.ws[:], T.wb[:])
+        act(("dj", "stp"), "tjs", T.tj[:, k:15 * n + k + 1:n], T.stp[:, 16 * k - 16:16 * k], F.Copy, scale=T.dj[:, k - 1:k])
+    do("v", V.tensor_tensor_scan, ("g", "dg"), "sgm", T.sgm[:], T.g[:], T.dg[:], BIG, A.min, A.max)
+    do("v", V.tensor_tensor, ("sgm",), "mn", T.mn[:], T.sgm[:, 14:256:16], T.sgm[:, 15:256:16], A.min)
+    do("v", V.tensor_scalar, ("mn", "jj"), "tj", T.tj[:, 0:15 * n + 1:n], T.mn[:], T.jj[:, 0:1], None, A.add)
+    do("v", V.tensor_tensor_scan, ("tj", "tjs", "rn"), "sj", T.sj[:, 0:16 * n], T.rn[:, 0:16 * n], T.tj[:, 0:16 * n], 0.0, A.mult, A.add)
+    do("v", V.tensor_copy, ("sj",), "fin", T.fin[:], T.sj[:, n - 1:16 * n:n])
 
     for b in (0, 1):
-        do("v", V.tensor_copy, ("dc", "own", "fin"), "t%d" % b, T.t2[:, 128 * b:128 * b + 128].bitcast(dt.uint32),
-           T.win[:].bitcast(dt.uint32).indirect(T.fin[:, 8 * b:8 * b + 8]))
-        do("s", S.activation, ("dsc", "own", "fin"), "t%ds" % b, T.t2s[:, 128 * b:128 * b + 128],
-           T.wins[:].indirect(T.fin[:, 8 * b:8 * b + 8]), F.Copy)
+        do("v", V.tensor_copy, ("dc", "own", "fin") + early, "t%d" % b, T.t2[:, 128 * b:128 * b + 128].bitcast(dt.uint32),
+           win[:].bitcast(dt.uint32).indirect(T.fin[:, 8 * b:8 * b + 8]))
+        act(("dsc", "own", "fin") + earlys, "t%ds" % b, T.t2s[:, 128 * b:128 * b + 128],
+            wins[:].indirect(T.fin[:, 8 * b:8 * b + 8]), F.Copy)
     for b in (0, 1):
         for o in (0, 1):
             k = 2 * b + o
@@ -387,14 +439,13 @@ def rank_program(g, core, T, topo):
                T.t2[:, 128 * b:128 * b + 128], T.t2s[:, 128 * b:128 * b + 128], True, True)
     for b in (0, 1):
         do("v", V.tensor_copy, ("mm%d" % (2 * b),), "y0", T.ysb[:, 128 * b:128 * b + 128], T.ps[:, 1024 * b:1024 * b + 128])
-        do("s", S.activation, ("mm%d" % (2 * b + 1),), "y1", T.ysb[:, P + 128 * b:P + 128 * b + 128],
-           T.ps[:, 1024 * b + 512:1024 * b + 640], F.Copy)
-    dma("y", ("y0",), "st0", "st0", T.y[:, 0:P], T.ysb[:, 0:P])
-    dma("s", ("y1",), "st9", "st9", T.y[:, P:2 * P], T.ysb[:, P:2 * P])
+        act(("mm%d" % (2 * b + 1),), "y1", T.ysb[:, P + 128 * b:P + 128 * b + 128], T.ps[:, 1024 * b + 512:1024 * b + 640], F.Copy)
+    dma("y", ("y0", "y1"), "st0", "st0", T.y[:], T.ysb[:])
 
     for q, s in own.items():
         ev["end_" + q] = (s, count[q])
     for s, v in final.items():
         ev["end_" + s] = (s, v)
     ev["end_ls"] = ("ls", nls)
-    need("g", *[k for k in ev if k.startswith("end_") or k.startswith("m1_")], "ls1", "m2", "dc", "dsc")
+    last = ["ls1", "m2", "dc", "dsc"] + list(early) + list(earlys)
+    need("g", *[k for k in ev if k.startswith("end_") or k.startswith("m1_")], *last)

@@ -203,6 +203,8 @@ def rank_program(g, core, T, topo):
     iota("i16", [[16, 8]])
     iota("fm", [[0, 17], [1, 16]])
     iota("et0", [[0, 1]], 0, T.et[:, 0:1])
+    iota("i800", [[16, 8]], NG)
+    iota("ik5", [[0, 2], [16, 6]])
     do("v", V.memset, (), "ones", T.ones[:], 1.0)
     do("v", V.memset, (), "mrk0", T.mrk[:, 0:NG], 0.0)
     do("v", V.tensor_scalar, ("ip",), "ipa", onei["ipa"], onei["ip"], 15, None, A.bitwise_and)
@@ -210,10 +212,12 @@ def rank_program(g, core, T, topo):
     do("v", V.tensor_copy, ("ipa",), "paf", paf, onei["ipa"])
     do("v", V.tensor_copy, ("ipg",), "pgf", one["pgf"], onei["ipg"])
     do("v", V.tensor_scalar, ("it8", "pgf"), "offc", T.offc[:], T.it8[:], one["pgf"], None, A.add)
+    do("v", V.memset, (), "mr0", T.mr2[:, SH:SH + P], 0.0)
     act(("paf",), "paf5", one["paf5"], paf, bias=0.5)
     act(("i16", "paf5"), "k8", T.k8[:], T.i16[:], bias=one["paf5"])
     act(("fm", "paf"), "fa", T.fa[:], T.fm[:, 1:257], F.Abs, bias=paf, scale=-1.0)
     act(("fa",), "dg", T.dg[:], T.fa[:], F.Relu, bias=BIG, scale=-BIG)
+    act(("i800", "paf"), "di8", T.di8[:], T.i800[:], bias=paf)
 
     mine = T.tot[:, 4 * r:4 * r + 1]
     do("v", V.tensor_copy, ("ct",), "tabf", T.tabf[:, 0:8], T.ct[:])
@@ -257,6 +261,10 @@ def rank_program(g, core, T, topo):
     dma("y", ("pk",), "l2own", "l2d", T.l2[:, o:o + 4], T.pk[:])
 
     do("v", V.quantize_mx, ("xb",), "xq", T.xq[:], T.xs[:], T.xb[:])
+    do("v", V.tensor_tensor, ("et", "di8"), "p1", T.p1[:, 0:8], T.et[:, 1:9], T.di8[:], A.subtract)
+    do("v", V.tensor_tensor, ("p1", "fl1"), "p2", T.p1[:, 8:16], T.p1[:, 0:8], T.fl1[:], A.mult)
+    do("v", V.tensor_tensor, ("p2", "di8"), "p3", T.p1[:, 16:24], T.p1[:, 8:16], T.di8[:], A.add)
+    do("v", V.tensor_copy, ("p3",), "pos8", T.pos8[:], T.p1[:, 16:24])
     do("v", V.tensor_scalar, ("cf",), "comp", T.comp[:], T.cf[:], 127.0, None, A.min)
     do("v", V.tensor_copy, ("xq", "comp"), "xc", T.xc[:].bitcast(dt.uint32), T.xq[:].bitcast(dt.uint32).indirect(T.comp[:, 0:8]))
     act(("xq", "comp"), "xcs", T.xcs[:], T.xs[:].indirect(T.comp[:, 0:8]), F.Copy)
@@ -268,21 +276,20 @@ def rank_program(g, core, T, topo):
                  for k, q in enumerate(dr)], "m2", "ls")
     dma("y", ("xc",), "own", "own", codes(win[:, 0:C]), codes(T.xc[:]))
     dma("y", ("xcs",), "own", "own", wins[:, 0:C], T.xcs[:])
+    do("v", V.tensor_copy, ("pos8", "ones", "mrk0"), "mrk", T.mrk[:].indirect(T.pos8[:]), T.ones[:, 0:128])
+    do("v", V.tensor_tensor_scan, ("mrk",), "grow", T.grow[:], T.mrk[:, 0:NG], T.mrk[:, 0:NG], 0.0, A.add, A.max)
+    do("v", V.quantize_mx, ("wb",), "wq", T.wq[:], T.ws[:], T.wb[:])
 
-    iota("i800", [[16, 8]], NG)
-    iota("ik5", [[0, 2], [16, 6]])
-    iota("idump", [[16, 40]], RG)
     iota("prz", [[0, 40]], -16, T.prx[:])
     iota("zm", [[0, 8]], -128)
+    iota("idump", [[16, 40]], RG)
     iota("fm8", [[0, 5], [1, 8]])
     iota("id8", [[1, 8]])
-    iota("mr0", [[0, P]], 0, T.mr2[:, SH:SH + P])
     for s in range(fi, hi + 1):
         if s != r and holder(s) != r:
             iota("bt", [[0, 1]], BASE[s - r], T.bt[:, s - fi:s - fi + 1])
     iota("ij", [[-128, n - 1], [16, 16]], SH - RG - 128, T.ij[:, 0:16 * n - 16])
     iota("fmn", [[0, 16], [1, n]], 0, T.fmn[:, 0:16 * n])
-    act(("i800", "paf"), "di8", T.di8[:], T.i800[:], bias=paf)
     act(("ik5", "paf"), "ik", T.ik[:], T.ik5[:], bias=paf)
     act(("paf",), "c55", one["a0"], paf, bias=-5.5)
     act(("paf",), "c11", one["a1"], paf, bias=-11.5)
@@ -294,23 +301,15 @@ def rank_program(g, core, T, topo):
     if up:
         kt = one["kt"]
         act(("kt", "tot"), "kt", kt, one["k2"], bias=mine)
-    act(("idump", "paf"), "di", T.di[:], T.idump[:], bias=paf)
     start = float(SH - RG + ((N - r) * P if up else -r * P))
-    act(("prz", "paf"), "pr0", T.prx[:, 0:1] if r < 3 else one["c0"], paf, scale=-1.0, bias=start)
     act(("paf",), "ca", one["ca"], paf, scale=129.0, bias=float(RG - SH))
+    act(("prz", "paf"), "pr0", T.prx[:, 0:1] if r < 3 else one["c0"], paf, scale=-1.0, bias=start)
+    act(("idump", "paf"), "di", T.di[:], T.idump[:], bias=paf)
     act(("fm8",), "rst8", T.rst8[:], T.fm8[:], F.Sign)
     act(("id8", "paf"), "da", T.da[:], T.id8[:], F.Abs, bias=paf, scale=-1.0)
     act(("da",), "dm", T.dm[:], T.da[:], F.Relu, bias=1.0, scale=-1.0)
     act(("ij",), "jh", T.jh[:, 0:16 * n - 16], T.ij[:, 0:16 * n - 16], bias=0.5)
     act(("fmn",), "rn", T.rn[:, 0:16 * n], T.fmn[:, 0:16 * n], F.Sign)
-
-    do("v", V.tensor_tensor, ("et", "di8"), "p1", T.p1[:, 0:8], T.et[:, 1:9], T.di8[:], A.subtract)
-    do("v", V.tensor_tensor, ("p1", "fl1"), "p2", T.p1[:, 8:16], T.p1[:, 0:8], T.fl1[:], A.mult)
-    do("v", V.tensor_tensor, ("p2", "di8"), "p3", T.p1[:, 16:24], T.p1[:, 8:16], T.di8[:], A.add)
-    do("v", V.tensor_copy, ("p3",), "pos8", T.pos8[:], T.p1[:, 16:24])
-    do("v", V.tensor_copy, ("pos8", "ones", "mrk0"), "mrk", T.mrk[:].indirect(T.pos8[:]), T.ones[:, 0:128])
-    do("v", V.tensor_tensor_scan, ("mrk",), "grow", T.grow[:], T.mrk[:, 0:NG], T.mrk[:, 0:NG], 0.0, A.add, A.max)
-    do("v", V.quantize_mx, ("wb",), "wq", T.wq[:], T.ws[:], T.wb[:])
 
     for s in range(N):
         for kind in ("hop1", "direct"):

@@ -2,49 +2,40 @@ from concourse.bass import DstId, RemoteDMATransfer
 from concourse.mybir import dt, AluOpType as A, AxisListType, ActivationFunctionType as F
 
 N, C, P, DS = 8, 128, 256, 80
-BASE = {0: 0, -1: 128, -2: 256, 2: 336, 1: 416}
-WIN = 544
+OFF = 16
+WIN = OFF + 5 * DS
 SH = 2048
-NG, ND = 784, 128
-RG = 4112
+DUMP = 4112
+TAB = DUMP + 4096 + 5 * C + 16
 BIG = 1.0e6
 
 f32, bf, i32, u16, u8, c4 = "float32", "bfloat16", "int32", "uint16", "uint8", "float8_e4m3fn_x4"
 SCRATCH = {}
 for _n, _w, _d in [
     ("one", 32, f32), ("onei", 8, i32),
-    ("ct", 8, i32), ("tabf", 40, f32), ("bcs", 40, f32), ("trs", 32, f32),
-    ("tot", 32, f32), ("it8", 8, f32), ("offc", 8, u16), ("fm", 272, f32), ("fa", 256, f32), ("dg", 256, f32),
-    ("fm8", 40, f32), ("rst8", 40, f32), ("i16", 8, f32), ("k8", 8, f32), ("ik5", 12, f32), ("ik", 12, f32),
-    ("ij", 64, f32), ("jh", 64, f32), ("di", 40, f32), ("di8", 8, f32), ("idump", 40, f32), ("i800", 8, f32), ("id8", 8, f32), ("da", 8, f32), ("dm", 8, f32),
-    ("bc", 128, f32), ("nrow", 128, f32), ("erow", 128, f32), ("nz", 128, f32), ("zrow", 128, f32),
-    ("se", 128, f32), ("et", 9, f32), ("fl8", 8, f32), ("fl1", 8, f32), ("de", 8, f32), ("vv", 8, f32), ("vh", 4, f32), ("pkf", 4, f32),
-    ("pk", 4, u16), ("junk", 1024, f32), ("acc", 8, f32), ("cf", 8, f32), ("comp", 8, u16),
-    ("p1", 24, f32), ("pos8", 8, u16), ("mrk", NG + ND, bf), ("ones", 640, bf), ("grow", NG, f32),
-    ("thr", 2, u16), ("lo", 16, f32),
-    ("lf", 12, f32), ("lst", 12, u16), ("lsp", 6, u16),
-    ("l2", 20, u16), ("wi", 20, i32), ("dei", 40, i32), ("fli", 40, i32), ("def_", 40, f32), ("zm", 8, f32),
-    ("prx", 40, f32), ("er", 40, f32), ("cd", 40, f32),
-    ("po", 40, f32), ("pos", 40, u16), ("mr2", RG + 640, bf), ("g", 256, f32), ("sgm", 256, f32), ("mn", 16, f32),
-    ("kk", 24, f32), ("ks", 96, f32), ("kx", 96, f32), ("kj", 48, f32),
-    ("st", 8, f32), ("sto", 2, u16), ("h", 16, f32), ("bt", 8, f32), ("jj", 8, f32), ("dj", 8, f32),
-    ("sgn", 64, f32), ("stp", 64, f32), ("fmn", 80, f32), ("rn", 80, f32), ("tj", 80, f32), ("sj", 80, f32), ("fin", 16, u16),
+    ("ct", 8, i32), ("tabf", 8, f32), ("tot", 32, f32), ("it8", 8, f32), ("offc", 8, u16),
+    ("fm", 272, f32), ("fa", 256, f32), ("dg", 256, f32), ("fm8", 40, f32), ("rst8", 40, f32),
+    ("i16", 8, f32), ("k8", 8, f32), ("ikh", 8, f32), ("ik2", 8, f32), ("idump", 40, f32), ("di", 40, f32),
+    ("pw", 8, f32), ("c5", 8, f32), ("kt5", 8, f32), ("thr", 8, f32),
+    ("bc", 128, f32), ("nrow", 128, f32), ("erow", 136, f32), ("nz", 128, f32), ("zrow", 128, f32),
+    ("se", 128, f32), ("et", 12, f32), ("fl8", 8, f32), ("de", 8, f32), ("vv", 8, f32), ("pkf", 8, f32), ("pk", 4, u16),
+    ("junk", 1024, f32), ("acc", 8, f32), ("comp", 8, u16), ("ce", 128, f32), ("junl", 5 * C, f32), ("junp", 8, f32),
+    ("lfa", 12, f32), ("lsa", 12, u16), ("lfb", 12, f32), ("lsb", 12, u16), ("lfo", 6, f32), ("lso", 6, u16),
+    ("l2", 20, u16), ("wi", 20, i32), ("dei", 40, i32), ("fli", 40, i32), ("def_", 40, f32), ("fd", 40, f32),
+    ("prx", 40, f32), ("er", 40, f32), ("po", 40, f32), ("pos", 40, u16),
+    ("slots", 5 * C, bf), ("mr2", TAB, bf), ("mk", 256, bf), ("g", 256, f32), ("sgm", 256, f32), ("mn", 16, f32),
+    ("fin", 16, u16),
     ("xb", 512, bf), ("xq", 128, c4), ("xs", 128, u8), ("xc", 128, c4), ("xcs", 128, u8),
-    ("sp", 80, c4), ("sps", 80, u8), ("t2", 256, c4), ("t2s", 256, u8),
+    ("spa", 2 * DS, c4), ("spas", 2 * DS, u8), ("spb", 2 * DS, c4), ("spbs", 2 * DS, u8),
+    ("win", WIN, c4), ("wins", WIN, u8), ("t2", 256, c4), ("t2s", 256, u8),
     ("wb", 2048, bf), ("wq", 512, c4), ("ws", 512, u8), ("ysb", 512, f32),
-    ("r1b", 1, f32), ("r2b", 4, u16), ("rcb", 128, c4), ("rsb", 128, u8),
+    ("r1b", 1, f32), ("r2b", 4, u16), ("rcb", DS, c4), ("rsb", DS, u8),
 ]:
     SCRATCH[_n] = ("sbuf", [128, _w], _d)
-ONE = {k: i for i, k in enumerate(["paf", "paf5", "pgf", "sg", "pa", "st1", "c0", "ca", "s1", "s2", "k1", "k2", "kt",
-                                   "a0", "a1", "a2", "b0", "b1", "b2", "lop0", "lop1", "lop2"])}
+ONE = {k: i for i, k in enumerate(["paf", "paf5", "paf2", "pgf", "sg", "pa", "ia", "a0", "a1", "a2", "a3", "a4"])}
 ONEI = {k: i for i, k in enumerate(["ip", "ipa", "ipg"])}
-for _k in range(N // 2):
-    SCRATCH["win%d" % _k] = ("sbuf", [128, WIN], c4)
-    SCRATCH["wins%d" % _k] = ("sbuf", [128, WIN], u8)
-    SCRATCH["dn%d" % _k] = ("sbuf", [128, 2 * DS], c4)
-    SCRATCH["dns%d" % _k] = ("sbuf", [128, 2 * DS], u8)
 SCRATCH["ps"] = ("psum", [128, 2048], f32)
-SEMAPHORES = (["cl", "xl", "wl", "l2d", "own", "vs", "ss", "ts", "gs", "ls", "ls1", "m2", "dc", "dsc", "ec", "es",
+SEMAPHORES = (["cl", "xl", "wl", "l2d", "vs", "ss", "ts", "gs", "ls", "m2", "dc", "dsc",
                "r1", "r2", "rc", "rsc", "st0"] + ["m1_%d" % s for s in range(N)])
 
 
@@ -52,8 +43,12 @@ def needs(q):
     return list(range(q)) if q < N // 2 else list(range(q + 1, N))
 
 
-def holder(r):
-    return r + 1 if r < N - 1 else r - 1
+def first(q):
+    return max(0, q - 2)
+
+
+def base(s, q):
+    return OFF + DS * (s - first(q))
 
 
 def plan(T, topo):
@@ -81,13 +76,13 @@ def part(es, k, n):
 
 
 def sender(g, core, T, topo):
-    def send(items, rsem, lsem):
+    def send(items, rsem):
         tr = []
         for dst, es, o, i in items:
             rid, pid = topo.addr(dst, core)
             tr.append(RemoteDMATransfer(dst_ids=[DstId(rid=rid, pnc=pid)], dma_engine_mask=mask_of(es),
                                         remote_sem=T.sem[rsem], src=i, dst=o))
-        g.remote_dma_fused(tr, local_sem=T.sem[lsem])
+        g.remote_dma_fused(tr, local_sem=T.sem["ls"])
         return sum(len(es) for _, es, _, _ in items)
     return send
 
@@ -96,41 +91,31 @@ def codes(v):
     return v.bitcast(dt.uint8)
 
 
-def slot(s, q):
-    return s - max(0, q - 2)
-
-
-def window(T, q):
-    return T["win%d" % (q // 2)], T["wins%d" % (q // 2)]
-
-
-def relay_program(g, core, T, topo, pl, r, first):
+def relay_program(g, core, T, topo, pl, r, isx):
     me = pl[r]
     send = sender(g, core, T, topo)
     n = 0
-    dsts = me["hop1"] if first else me["hop"]
-    g.wait_ge(T.sem["r1" if first else "r2"], 8)
+    dsts = me["hop1"] if isx else me["hop"]
+    g.wait_ge(T.sem["r1" if isx else "r2"], 8)
     it = []
     for k, q in enumerate(dsts):
         dst = T.cores[q]
         es = part(topo.engines(core, dst), k, len(dsts))
-        if first:
+        if isx:
             it.append((dst, es, T.tot[:, 4 * r:4 * r + 1], T.r1b[:]))
         else:
-            o = 4 * slot(r, q)
+            o = 4 * (r - first(q))
             it.append((dst, es, T.l2[:, o:o + 4], T.r2b[:]))
-    n += send(it, "m1_%d" % r if first else "m2", "ls")
-    q = holder(r)
-    dst = T.cores[q]
-    es = topo.engines(core, dst)
-    b = BASE[r - q]
-    win, wins = window(T, q)
-    if first:
-        g.wait_ge(T.sem["rsc"], 16)
-        n += send([(dst, es, wins[:, b:b + C], T.rsb[:])], "es", "ls")
-    else:
-        g.wait_ge(T.sem["rc"], 16)
-        n += send([(dst, es, codes(win[:, b:b + C]), codes(T.rcb[:]))], "ec", "ls")
+    n += send(it, "m1_%d" % r if isx else "m2")
+    for k, q in enumerate(me["hop"]):
+        if (k == 0) == isx:
+            dst = T.cores[q]
+            es = topo.engines(core, dst)
+            b = base(r, q)
+            g.wait_ge(T.sem["rc"], 8)
+            n += send([(dst, es, codes(T.win[:, b:b + DS]), codes(T.rcb[:]))], "dc")
+            g.wait_ge(T.sem["rsc"], 8)
+            n += send([(dst, es, T.wins[:, b:b + DS], T.rsb[:])], "dsc")
     g.wait_ge(T.sem["ls"], n)
 
 
@@ -178,12 +163,17 @@ def rank_program(g, core, T, topo):
     one = {k: T.one[:, i:i + 1] for k, i in ONE.items()}
     onei = {k: T.onei[:, i:i + 1] for k, i in ONEI.items()}
     paf = one["paf"]
-    win, wins = window(T, r)
-    dn, dns = T["dn%d" % (r // 2)], T["dns%d" % (r // 2)]
     up = r >= N // 2
-    fi, hi = max(0, r - 2), min(N - 1, r + 2)
+    fi, hi = first(r), min(N - 1, r + 2)
     n = hi - fi + 1
     m = 8 * n
+
+    def iota(name, pattern, base_=0, out=None, reads=()):
+        do("g", g.iota, reads, name, T[name][:] if out is None else out, pattern, base_, 0,
+           allow_small_or_imprecise_dtypes=True)
+
+    def act(reads, write, out, in_, func=F.Identity, **kw):
+        do("s", S.activation, reads, write, out, in_, func, **kw)
 
     for k in range(4):
         for q, j in (("y", 2 * k), ("s", 2 * k + 1)):
@@ -191,22 +181,16 @@ def rank_program(g, core, T, topo):
     dma("y", (), "xb", "xl", T.xb[:], T.x[:])
     dma("y", (), "wb", "wl", T.wb[:], T.w[:])
 
-    def iota(name, pattern, base=0, out=None):
-        do("g", g.iota, (), name, T[name][:] if out is None else out, pattern, base, 0, allow_small_or_imprecise_dtypes=True)
-
-    def act(reads, write, out, in_, func=F.Identity, **kw):
-        do("s", S.activation, reads, write, out, in_, func, **kw)
-    z32 = T.tabf[:, 8:40]
     do("g", g.iota, (), "ip", onei["ip"], [[1, 1]], 0, 1)
-    iota("z32", [[0, 32]], 0, z32)
     iota("it8", [[2, 4], [0, 2]])
-    iota("i16", [[16, 8]])
     iota("fm", [[0, 17], [1, 16]])
+    iota("er0", [[0, 1]], 0, T.erow[:, 7:8])
     iota("et0", [[0, 1]], 0, T.et[:, 0:1])
-    iota("i800", [[16, 8]], NG)
-    iota("ik5", [[0, 2], [16, 6]])
-    do("v", V.memset, (), "ones", T.ones[:], 1.0)
-    do("v", V.memset, (), "mrk0", T.mrk[:, 0:NG], 0.0)
+    iota("i16", [[16, 8]])
+    iota("pw", [[0, 4], [256, 2]])
+    iota("c5", [[P, 5]], (r - 2) * P - (N * P if up else 0), T.c5[:, 0:5])
+    for k in range(n):
+        do("v", V.memset, (), "slots", T.slots[:, C * k:C * k + C], float(OFF + DS * k))
     do("v", V.tensor_scalar, ("ip",), "ipa", onei["ipa"], onei["ip"], 15, None, A.bitwise_and)
     do("v", V.tensor_scalar, ("ip",), "ipg", onei["ipg"], onei["ip"], 4, 1, A.logical_shift_right, A.bitwise_and)
     do("v", V.tensor_copy, ("ipa",), "paf", paf, onei["ipa"])
@@ -217,219 +201,165 @@ def rank_program(g, core, T, topo):
     act(("i16", "paf5"), "k8", T.k8[:], T.i16[:], bias=one["paf5"])
     act(("fm", "paf"), "fa", T.fa[:], T.fm[:, 1:257], F.Abs, bias=paf, scale=-1.0)
     act(("fa",), "dg", T.dg[:], T.fa[:], F.Relu, bias=BIG, scale=-BIG)
-    act(("i800", "paf"), "di8", T.di8[:], T.i800[:], bias=paf)
 
-    mine = T.tot[:, 4 * r:4 * r + 1]
-    do("v", V.tensor_copy, ("ct",), "tabf", T.tabf[:, 0:8], T.ct[:])
-    do("v", V.tensor_tensor_scan, ("tabf", "z32"), "bcs", T.bcs[:], T.tabf[:], T.tabf[:], 0.0, A.add, A.max)
-    do("v", V.transpose, ("bcs",), "trs", T.trs[:], T.bcs[:, 8:40])
-    do("v", V.tensor_reduce, ("trs",), "tot", mine, T.trs[:, 0:16], X, A.add)
+    end = T.erow[:, 8:136]
+    mine = T.erow[:, 135:136]
+    do("v", V.tensor_copy, ("ct", "offc"), "bc", T.bc[:], T.ct[:, 0:8].indirect(T.offc[:]))
+    do("v", V.transpose, ("bc",), "nrow", T.nrow[:], T.bc[:])
+    act(("nrow",), "nz", T.nz[:], T.nrow[:], F.Sign)
+    do("v", V.tensor_tensor_scan, ("nrow",), "erow", end, T.nrow[:], T.nrow[:], 0.0, A.add, A.max)
 
-    nls1, nls = 0, 0
-    need("g", "tot")
-    chip, chipy = topo.engines(core, me["X"]), topo.engines(core, me["Y"])
-    nls1 += send([(me["X"], part(chip, 0, 2), T.r1b[:], mine)], "r1", "ls1")
-    dr = me["direct"]
+    nls = 0
+    need("g", "erow")
+    chip, chipy = part(topo.engines(core, me["X"]), 0, 2), part(topo.engines(core, me["Y"]), 1, 2)
+    dr, hop = me["direct"], me["hop"]
 
     def direct_engines(k):
         return part(topo.engines(core, T.cores[dr[k]]), k, len(dr))
-    nls1 += send([(T.cores[q], direct_engines(k), mine, mine) for k, q in enumerate(dr)], "m1_%d" % r, "ls1")
-    ev["ls1"] = ("ls1", nls1)
+    nls += send([(me["X"], chip, T.r1b[:], mine)], "r1")
+    nls += send([(T.cores[q], direct_engines(k), T.tot[:, 4 * r:4 * r + 1], mine) for k, q in enumerate(dr)], "m1_%d" % r)
 
-    do("v", V.tensor_copy, ("tabf", "offc"), "bc", T.bc[:], T.tabf[:, 0:8].indirect(T.offc[:]))
-    do("v", V.transpose, ("bc",), "nrow", T.nrow[:], T.bc[:])
-    act(("nrow",), "nz", T.nz[:], T.nrow[:], F.Sign)
-    act(("tabf",), "fl1", T.fl1[:], T.tabf[:, 0:8], F.Sign)
-    act(("fl1",), "fl8", T.fl8[:], T.fl1[:], F.Copy, scale=128.0)
-    do("v", V.tensor_tensor_scan, ("nrow",), "erow", T.erow[:], T.nrow[:], T.nrow[:], 0.0, A.add, A.max)
+    do("v", V.tensor_tensor_scan, ("erow", "er0", "dg"), "se", T.se[:], T.erow[:, 7:135], T.dg[:, 0:128], BIG, A.min, A.max)
     do("v", V.tensor_tensor_scan, ("nz",), "zrow", T.zrow[:], T.nz[:], T.nz[:], 0.0, A.add, A.max)
+    do("v", V.tensor_copy, ("ct",), "tabf", T.tabf[:], T.ct[:])
+    act(("tabf",), "fl8", T.fl8[:], T.tabf[:], F.Relu, scale=-128.0, bias=128.0)
     for c in range(8):
-        act(("zrow", "k8"), "acc", T.junk[:, 128 * c:128 * c + 128], T.zrow[:], F.Sign,
+        act(("zrow", "k8"), "acc", T.junk[:, 128 * c:128 * c + 127], T.zrow[:, 0:127], F.Sign,
             bias=T.k8[:, c:c + 1], scale=-1.0, accum_out=T.acc[:, c:c + 1])
-    act(("acc",), "cf", T.cf[:], T.acc[:], bias=64.0, scale=0.5)
-    do("v", V.tensor_tensor_scan, ("erow", "dg"), "se", T.se[:], T.erow[:], T.dg[:, 0:128], BIG, A.min, A.max)
     do("v", V.tensor_tensor, ("se",), "et", T.et[:, 1:9], T.se[:, 14:128:16], T.se[:, 15:128:16], A.min)
     do("v", V.tensor_tensor, ("et", "et0"), "de", T.de[:], T.et[:, 1:9], T.et[:, 0:8], A.subtract)
     do("v", V.tensor_tensor, ("de", "fl8"), "vv", T.vv[:], T.de[:], T.fl8[:], A.add)
-    do("v", V.tensor_scalar, ("vv",), "vh", T.vh[:], T.vv[:, 1:8:2], 256.0, None, A.mult)
-    do("v", V.tensor_tensor, ("vv", "vh"), "pkf", T.pkf[:], T.vv[:, 0:8:2], T.vh[:], A.add)
-    do("v", V.tensor_copy, ("pkf",), "pk", T.pk[:], T.pkf[:])
+    do("v", V.tensor_tensor_scan, ("vv", "pw"), "pkf", T.pkf[:], T.pw[:], T.vv[:], 0.0, A.mult, A.add)
+    do("v", V.tensor_copy, ("pkf",), "pk", T.pk[:], T.pkf[:, 1:8:2])
 
     need("g", "pk")
-    nls += send([(me["Y"], part(chipy, 1, 2), T.r2b[:], T.pk[:])], "r2", "ls")
-    o = 4 * slot(r, r)
+    nls += send([(me["Y"], chipy, T.r2b[:], T.pk[:])], "r2")
+    nls += send([(T.cores[q], direct_engines(k), T.l2[:, 4 * (r - first(q)):4 * (r - first(q)) + 4], T.pk[:])
+                 for k, q in enumerate(dr)], "m2")
+    o = 4 * (r - fi)
     dma("y", ("pk",), "l2own", "l2d", T.l2[:, o:o + 4], T.pk[:])
 
     do("v", V.quantize_mx, ("xb",), "xq", T.xq[:], T.xs[:], T.xb[:])
-    do("v", V.tensor_tensor, ("et", "di8"), "p1", T.p1[:, 0:8], T.et[:, 1:9], T.di8[:], A.subtract)
-    do("v", V.tensor_tensor, ("p1", "fl1"), "p2", T.p1[:, 8:16], T.p1[:, 0:8], T.fl1[:], A.mult)
-    do("v", V.tensor_tensor, ("p2", "di8"), "p3", T.p1[:, 16:24], T.p1[:, 8:16], T.di8[:], A.add)
-    do("v", V.tensor_copy, ("p3",), "pos8", T.pos8[:], T.p1[:, 16:24])
-    do("v", V.tensor_scalar, ("cf",), "comp", T.comp[:], T.cf[:], 127.0, None, A.min)
+    do("v", V.tensor_scalar, ("acc",), "comp", T.comp[:], T.acc[:], 0.5, 63.5, A.mult, A.add)
     do("v", V.tensor_copy, ("xq", "comp"), "xc", T.xc[:].bitcast(dt.uint32), T.xq[:].bitcast(dt.uint32).indirect(T.comp[:, 0:8]))
+    act(("erow", "comp"), "ce", T.ce[:], end.indirect(T.comp[:, 0:8]), F.Copy)
+    act(("erow",), "tot", T.tot[:, 4 * r:4 * r + 1], mine, F.Copy)
     act(("xq", "comp"), "xcs", T.xcs[:], T.xs[:].indirect(T.comp[:, 0:8]), F.Copy)
-    need("g", "xc")
-    nls += send([(me["Y"], chipy, codes(T.rcb[:]), codes(T.xc[:]))], "rc", "ls")
-    need("g", "xcs")
-    nls += send([(me["X"], chip, T.rsb[:], T.xcs[:])], "rsc", "ls")
-    nls += send([(T.cores[q], direct_engines(k), T.l2[:, 4 * slot(r, q):4 * slot(r, q) + 4], T.pk[:])
-                 for k, q in enumerate(dr)], "m2", "ls")
-    dma("y", ("xc",), "own", "own", codes(win[:, 0:C]), codes(T.xc[:]))
-    dma("y", ("xcs",), "own", "own", wins[:, 0:C], T.xcs[:])
-    do("v", V.tensor_copy, ("pos8", "ones", "mrk0"), "mrk", T.mrk[:].indirect(T.pos8[:]), T.ones[:, 0:128])
-    do("v", V.tensor_tensor_scan, ("mrk",), "grow", T.grow[:], T.mrk[:, 0:NG], T.mrk[:, 0:NG], 0.0, A.add, A.max)
     do("v", V.quantize_mx, ("wb",), "wq", T.wq[:], T.ws[:], T.wb[:])
 
-    iota("prz", [[0, 40]], -16, T.prx[:])
-    iota("zm", [[0, 8]], -128)
-    iota("idump", [[16, 40]], RG)
+    iota("ikh", [[16, 8]])
+    iota("prz", [[0, 40]], 0, T.prx[:])
+    iota("idump", [[16, 40]], DUMP)
     iota("fm8", [[0, 5], [1, 8]])
-    iota("id8", [[1, 8]])
-    for s in range(fi, hi + 1):
-        if s != r and holder(s) != r:
-            iota("bt", [[0, 1]], BASE[s - r], T.bt[:, s - fi:s - fi + 1])
-    iota("ij", [[-128, n - 1], [16, 16]], SH - RG - 128, T.ij[:, 0:16 * n - 16])
-    iota("fmn", [[0, 16], [1, n]], 0, T.fmn[:, 0:16 * n])
-    act(("ik5", "paf"), "ik", T.ik[:], T.ik5[:], bias=paf)
-    act(("paf",), "c55", one["a0"], paf, bias=-5.5)
-    act(("paf",), "c11", one["a1"], paf, bias=-11.5)
-    act(("c55",), "s1", one["s1"], one["a0"], F.Sign)
-    act(("c11",), "s2", one["s2"], one["a1"], F.Sign)
-    act(("s1",), "k1", one["k1"], one["s1"], scale=float(-2 * P), bias=float((r + 1) * P - (N * P if up else 0)))
-    act(("s2", "k1"), "kt", one["k2"], one["s2"], scale=float(P), bias=one["k1"])
-    kt = one["k2"]
-    if up:
-        kt = one["kt"]
-        act(("kt", "tot"), "kt", kt, one["k2"], bias=mine)
-    start = float(SH - RG + ((N - r) * P if up else -r * P))
-    act(("paf",), "ca", one["ca"], paf, scale=129.0, bias=float(RG - SH))
-    act(("prz", "paf"), "pr0", T.prx[:, 0:1] if r < 3 else one["c0"], paf, scale=-1.0, bias=start)
+    if r < 3:
+        iota("pr0", [[0, 1]], SH - r * P, T.prx[:, 0:1], reads=("prz",))
+    act(("paf",), "paf2", one["paf2"], paf, scale=2.0, bias=127.0)
+    act(("ikh", "paf2"), "ik2", T.ik2[:], T.ikh[:], scale=2.0, bias=one["paf2"])
     act(("idump", "paf"), "di", T.di[:], T.idump[:], bias=paf)
     act(("fm8",), "rst8", T.rst8[:], T.fm8[:], F.Sign)
-    act(("id8", "paf"), "da", T.da[:], T.id8[:], F.Abs, bias=paf, scale=-1.0)
-    act(("da",), "dm", T.dm[:], T.da[:], F.Relu, bias=1.0, scale=-1.0)
-    act(("ij",), "jh", T.jh[:, 0:16 * n - 16], T.ij[:, 0:16 * n - 16], bias=0.5)
-    act(("fmn",), "rn", T.rn[:, 0:16 * n], T.fmn[:, 0:16 * n], F.Sign)
+    kt, ktk = T.c5[:, 0:5], "c5"
+    if up:
+        act(("c5", "erow"), "kt5", T.kt5[:, 0:5], T.c5[:, 0:5], bias=mine)
+        kt, ktk = T.kt5[:, 0:5], "kt5"
 
+    n2, nd = 0, 0
     for s in range(N):
         for kind in ("hop1", "direct"):
             if r in pl[s][kind]:
                 ev["m1_%d" % s] = ("m1_%d" % s, 8 // len(pl[s][kind]))
-    n2, nd, ne = 0, 0, 0
-    for s in range(N):
         if r in pl[s]["hop"]:
             n2 += 8 // len(pl[s]["hop"])
+            nd += 8
         elif r in pl[s]["direct"]:
             n2 += 8 // len(pl[s]["direct"])
-            nd += 8
-        if holder(s) == r:
-            ne += 8
+            nd += 8 // len(pl[s]["direct"])
     ev["m2"], ev["dc"], ev["dsc"] = ("m2", n2), ("dc", nd), ("dsc", nd)
-    early, earlys = (), ()
-    if ne:
-        ev["ec"], ev["es"] = ("ec", ne), ("es", ne)
-        early, earlys = ("ec",), ("es",)
-    held = [s for s in range(N) if holder(s) == r]
 
-    ns = [] if r in (0, N - 1) else needs(r)
+    ns = needs(r)
     keys = ["m1_%d" % s for s in ns]
     if not ns:
-        do("v", V.tensor_scalar, ("kt",), "thr", T.thr[:, 0:1], kt, 768.0, None, A.min)
+        do("v", V.tensor_scalar, (ktk,), "thr", T.thr[:, 0:5], kt, 0.5, None, A.add)
     else:
         sg = T.tot[:, 4 * ns[0]:4 * ns[0] + 1]
         if len(ns) > 1:
             do("v", V.tensor_reduce, keys, "sg", one["sg"], T.tot[:, 4 * ns[0]:4 * ns[-1] + 1:4], X, A.add)
             sg, keys = one["sg"], ["sg"]
-        do("v", V.tensor_scalar, ["kt"] + keys, "thr", T.thr[:, 0:1], kt, sg, 768.0, A.add if up else A.subtract, A.min)
-    do("v", V.tensor_copy, ("thr", "grow"), "lo", T.lo[:], T.grow[:].indirect(T.thr[:, 0:1]))
-    do("v", V.tensor_tensor, ("lo", "ik"), "lf", T.lf[:], T.lo[:, 0:12], T.ik[:], A.add)
-    do("v", V.tensor_scalar, ("lf",), "lst", T.lst[:], T.lf[:], 127.0, None, A.min)
-
-    def pick(name, dst, dsts, list_, lkey, src, srcs, keys, skeys):
-        do("v", V.tensor_copy, (lkey,) + keys, name, dst.bitcast(dt.uint32), src.bitcast(dt.uint32).indirect(list_))
-        act((lkey,) + skeys, name + "s", dsts, srcs.indirect(list_), F.Copy)
-
-    def late(q, src, srcs, w, kc, ks):
-        b = BASE[r - q]
-        to, tos = window(T, q)
-        es = topo.engines(core, T.cores[q])
-        need("g", *kc)
-        a = send([(T.cores[q], es, codes(to[:, b:b + w]), codes(src[:, 0:w]))], "dc", "ls")
-        need("g", *ks)
-        return a + send([(T.cores[q], es, tos[:, b:b + w], srcs[:, 0:w])], "dsc", "ls")
-    if r + 2 < N:
-        pick("snd0", T.sp[:, 0:DS], T.sps[:, 0:DS], T.lst[:, 0:5], "lst", T.xc[:, 0:C], T.xcs[:, 0:C], ("xc",), ("xcs",))
-        nls += late(r + 2, T.sp, T.sps, DS, ("snd0",), ("snd0s",))
-    if r >= 2:
-        pick("snd1", dn[:, 0:DS], dns[:, 0:DS], T.lst[:, 6:11], "lst", T.xc[:, 0:C], T.xcs[:, 0:C], ("xc",), ("xcs",))
-    act(("lo",), "bts", T.bt[:, r - fi:r - fi + 1], T.lo[:, 12:13], F.Copy, bias=float(BASE[0]))
+        do("v", V.tensor_scalar, [ktk] + keys, "thr", T.thr[:, 0:5], kt, sg, 0.5, A.add if up else A.subtract, A.add)
 
     if r == 3:
-        do("v", V.tensor_scalar, ("prz", "pr0", "m1_0"), "pr0", T.prx[:, 0:1], T.tot[:, 0:1], one["c0"], None, A.add)
+        do("v", V.tensor_scalar, ("prz", "m1_0"), "pr0", T.prx[:, 0:1], T.tot[:, 0:1], float(SH - r * P), None, A.add)
     elif up:
         do("v", V.tensor_reduce, ["m1_%d" % s for s in range(fi, N) if s != r] + ["tot"], "pa", one["pa"],
            T.tot[:, 4 * fi:4 * (N - 1) + 1:4], X, A.add)
-        do("v", V.tensor_scalar, ("prz", "pr0", "pa"), "pr0", T.prx[:, 0:1], one["pa"], -1.0, one["c0"], A.mult, A.add)
-    do("v", V.tensor_tensor_scan, ["m1_%d" % s for s in range(fi, hi) if s != r] + ["tot", "zm", "pr0", "prz"], "prx",
-       T.prx[:, 8:8 * (n - 1) + 1:8], T.tot[:, 4 * fi:4 * (hi - 1) + 1:4], T.zm[:, 0:n - 1], T.prx[:, 0:1], A.add, A.add)
-    for k in range(1, n):
-        act(("prx", "jh"), "sgn", T.sgn[:, 16 * k - 16:16 * k], T.jh[:, 16 * k - 16:16 * k], F.Sign,
-            bias=T.prx[:, 8 * k:8 * k + 1], scale=-1.0)
-    act(("sgn",), "stp", T.stp[:, 0:16 * n - 16], T.sgn[:, 0:16 * n - 16], F.Relu, scale=-1.0)
+        do("v", V.tensor_scalar, ("prz", "pa"), "pr0", T.prx[:, 0:1], one["pa"], -1.0, float(SH + (N - r) * P), A.mult, A.add)
+    steps = T.tot[:, 4 * fi:4 * (hi - 1) + 1:4]
+    do("v", V.tensor_tensor_scan, ["m1_%d" % s for s in range(fi, hi) if s != r] + ["tot", "pr0", "prz"], "prx",
+       T.prx[:, 8:8 * (n - 1) + 1:8], steps, steps, T.prx[:, 0:1], A.add, A.max)
+
+    def lists(dsts, lf, ls, name):
+        for i, q in enumerate(dsts):
+            d = q - (r - 2)
+            act(("ce", "thr"), "a%d" % d, T.junl[:, C * d:C * d + 127], T.ce[:, 0:127], F.Sign,
+                bias=T.thr[:, d:d + 1], scale=-1.0, accum_out=one["a%d" % d])
+        for i, q in enumerate(dsts):
+            d = q - (r - 2)
+            act(("ik2", "a%d" % d), name + "f", lf[:, 5 * i:5 * i + 5], T.ik2[:, 0:5], bias=one["a%d" % d])
+
+    def clamp(k, lf, ls, name):
+        do("v", V.tensor_scalar, (name + "f",), name, ls[:, 0:5 * k], lf[:, 0:5 * k], 0.5, 127.0, A.mult, A.min)
+
+    def pick(k, dst, dsts, ls, name):
+        do("v", V.tensor_copy, ("xc", name), name + "c", dst.bitcast(dt.uint32), T.xc[:].bitcast(dt.uint32).indirect(ls[:, 0:5 * k]))
+        act(("xcs", name), name + "s", dsts, T.xcs[:].indirect(ls[:, 0:5 * k]), F.Copy)
+    ka, kb = len(hop), len(dr)
+    lists(hop, T.lfa, T.lsa, "la")
+    clamp(ka, T.lfa, T.lsa, "la")
+    pick(ka, T.spa[:, 0:DS * ka], T.spas[:, 0:DS * ka], T.lsa, "la")
+    relay = [(me["X"], chip), (me["Y"], chipy)]
+    need("g", "lac")
+    nls += send([(c, es, codes(T.rcb[:]), codes(T.spa[:, DS * i:DS * i + DS])) for i, (c, es) in enumerate(relay[:ka])], "rc")
+    need("g", "las")
+    nls += send([(c, es, T.rsb[:], T.spas[:, DS * i:DS * i + DS]) for i, (c, es) in enumerate(relay[:ka])], "rsc")
+    lists(dr, T.lfb, T.lsb, "lb")
+    clamp(kb, T.lfb, T.lsb, "lb")
+    pick(kb, T.spb[:, 0:DS * kb], T.spbs[:, 0:DS * kb], T.lsb, "lb")
+    need("g", "lbc")
+    nls += send([(T.cores[q], direct_engines(i), codes(T.win[:, base(r, q):base(r, q) + DS]), codes(T.spb[:, DS * i:DS * i + DS]))
+                 for i, q in enumerate(dr)], "dc")
+    need("g", "lbs")
+    nls += send([(T.cores[q], direct_engines(i), T.wins[:, base(r, q):base(r, q) + DS], T.spbs[:, DS * i:DS * i + DS])
+                 for i, q in enumerate(dr)], "dsc")
+    lists([r], T.lfo, T.lso, "lo")
+
     do("v", V.tensor_copy, ("m2", "l2own"), "wi", T.wi[:, 0:4 * n], T.l2[:, 0:4 * n])
     wi = T.wi[:, 0:4 * n]
-    do("v", V.tensor_scalar, ("wi",), "dei", T.dei[:, 0:m:2], wi, 127, None, A.bitwise_and)
-    do("v", V.tensor_scalar, ("wi",), "dei2", T.dei[:, 1:m:2], wi, 8, 127, A.logical_shift_right, A.bitwise_and)
-    do("v", V.tensor_scalar, ("wi",), "fli", T.fli[:, 0:m:2], wi, 7, 1, A.logical_shift_right, A.bitwise_and)
-    do("v", V.tensor_scalar, ("wi",), "fli2", T.fli[:, 1:m:2], wi, 15, None, A.logical_shift_right)
+    do("v", V.tensor_scalar, ("wi",), "dei", T.dei[:, 1:m:2], wi, 127, None, A.bitwise_and)
+    do("v", V.tensor_scalar, ("wi",), "dei2", T.dei[:, 0:m:2], wi, 8, 127, A.logical_shift_right, A.bitwise_and)
+    do("v", V.tensor_scalar, ("wi",), "fli", T.fli[:, 1:m:2], wi, 7, 1, A.logical_shift_right, A.bitwise_and)
+    do("v", V.tensor_scalar, ("wi",), "fli2", T.fli[:, 0:m:2], wi, 15, None, A.logical_shift_right)
     do("v", V.tensor_tensor, ("dei2", "prx"), "def_", T.def_[:, 0:m], T.dei[:, 0:m], T.prx[:, 0:m], A.add)
+    do("v", V.tensor_tensor, ("fli2", "di"), "fd", T.fd[:, 0:m], T.fli[:, 0:m], T.di[:, 0:m], A.mult)
     do("v", V.tensor_tensor_scan, ("def_", "rst8"), "er", T.er[:, 0:m], T.rst8[:, 0:m], T.def_[:, 0:m], 0.0, A.mult, A.add)
-    do("v", V.tensor_tensor, ("er", "fli2"), "cd", T.cd[:, 0:m], T.er[:, 0:m], T.fli[:, 0:m], A.mult)
-    do("v", V.tensor_tensor, ("cd", "di"), "po", T.po[:, 0:m], T.cd[:, 0:m], T.di[:, 0:m], A.add)
-
-    jobs = [(r - 1, r - 2)] if r >= 2 else []
-    jobs += [(s, r) for s in held]
-    for k, (s, q) in enumerate(jobs):
-        b = 8 * slot(s, r)
-        act(("po", "ca"), "pq%d" % k, T.kj[:, 8 * k:8 * k + 8], T.po[:, b:b + 8], scale=-1.0, bias=float(SH + (q - r) * P) + 0.5)
-        act(("pq%d" % k,), "a%d" % k, T.kk[:, 8 * k:8 * k + 8], T.kj[:, 8 * k:8 * k + 8], F.Sign, accum_out=one["a%d" % k])
-        act(("a%d" % k,), "b%d" % k, one["b%d" % k], one["a%d" % k], scale=0.5, bias=4.0)
-        act(("b%d" % k, "z32"), "ks%d" % k, T.ks[:, 32 * k:32 * k + 32], z32, bias=one["b%d" % k])
+    clamp(1, T.lfo, T.lso, "lo")
+    do("v", V.tensor_tensor, ("er", "fd"), "po", T.po[:, 0:m], T.er[:, 0:m], T.fd[:, 0:m], A.add)
+    b = base(r, r)
+    pick(1, T.win[:, b:b + DS], T.wins[:, b:b + DS], T.lso, "lo")
     do("v", V.tensor_copy, ("po",), "pos", T.pos[:, 0:m], T.po[:, 0:m])
-    do("v", V.tensor_tensor, ("prx", "dm"), "st", T.st[:, 0:n], T.prx[:, 0:m:8], T.dm[:, 0:n], A.mult)
-    do("v", V.tensor_reduce, ("st",), "st1", one["st1"], T.st[:, 0:n], X, A.add)
-    do("v", V.tensor_scalar, ("st1", "ca"), "sto", T.sto[:, 0:1], one["st1"], one["ca"], 255.0, A.add, A.min)
-    if r >= 2:
-        do("v", V.transpose, ("ks0",), "kx0", T.kx[:, 0:32], T.ks[:, 0:32])
-        do("v", V.tensor_reduce, ("kx0",), "lop0", one["lop0"], T.kx[:, 0:16], X, A.add)
-        do("v", V.tensor_scalar, ("lop0", "ik"), "lsp", T.lsp[:, 0:5], T.ik[:, 0:5], one["lop0"], 127.0, A.add, A.min)
-        b = BASE[-1]
-        pick("snd2", dn[:, DS:2 * DS], dns[:, DS:2 * DS], T.lsp[:, 0:5], "lsp", win[:, b:b + C], wins[:, b:b + C], early, earlys)
-        nls += late(r - 2, dn, dns, 2 * DS, ("snd1", "snd2"), ("snd1s", "snd2s"))
-    for k, (s, q) in enumerate(jobs):
-        if q == r:
-            do("v", V.transpose, ("ks%d" % k,), "kx%d" % k, T.kx[:, 32 * k:32 * k + 32], T.ks[:, 32 * k:32 * k + 32])
-            act(("kx%d" % k,), "lop%d" % k, T.junk[:, 16 * k:16 * k + 16], T.kx[:, 32 * k:32 * k + 16], F.Copy, accum_out=one["lop%d" % k])
-            act(("lop%d" % k,), "bts", T.bt[:, s - fi:s - fi + 1], one["lop%d" % k], F.Copy, bias=float(BASE[s - r]))
+    act(("prx",), "ia", T.junp[:, 0:n - 1], T.prx[:, 8:8 * (n - 1) + 1:8], F.Sign, scale=-1.0, bias=SH + 0.5, accum_out=one["ia"])
+    act(("ia",), "g0", T.g[:, 0:1], one["ia"], scale=DS / 2.0, bias=float(OFF + DS * (n - 1) // 2))
 
-    do("v", V.tensor_copy, ("pos", "ones", "mr0"), "mr2", T.mr2[:].indirect(T.pos[:, 0:m]), T.ones[:, 0:16 * m])
-    do("v", V.tensor_tensor_scan, ("mr2",), "g", T.g[:], T.mr2[:, SH:SH + P], T.mr2[:, SH:SH + P], 0.0, A.add, A.max)
-    do("v", V.tensor_copy, ("sto", "g"), "h", T.h[:], T.g[:].indirect(T.sto[:, 0:1]))
-    do("v", V.tensor_tensor, ("h", "bt", "bts"), "jj", T.jj[:, 0:n], T.bt[:, 0:n], T.h[:, 0:n], A.subtract)
-    do("v", V.tensor_tensor, ("jj",), "dj", T.dj[:, 0:n - 1], T.jj[:, 1:n], T.jj[:, 0:n - 1], A.subtract)
-    for k in range(1, n):
-        act(("dj", "stp"), "tjs", T.tj[:, k:15 * n + k + 1:n], T.stp[:, 16 * k - 16:16 * k], F.Copy, scale=T.dj[:, k - 1:k])
+    do("v", V.tensor_copy, ("pos", "slots", "mr0"), "mr2", T.mr2[:].indirect(T.pos[:, 0:m]), T.slots[:, 0:16 * m])
+    do("v", V.tensor_scalar, ("mr2",), "mk", T.mk[:], T.mr2[:, SH:SH + P], 0.0, None, A.is_gt)
+    do("v", V.tensor_tensor_scan, ("mk", "g0"), "g", T.g[:, 1:P], T.mk[:, 1:P], T.mr2[:, SH + 1:SH + P], T.g[:, 0:1], A.add, A.max)
     do("v", V.tensor_tensor_scan, ("g", "dg"), "sgm", T.sgm[:], T.g[:], T.dg[:], BIG, A.min, A.max)
     do("v", V.tensor_tensor, ("sgm",), "mn", T.mn[:], T.sgm[:, 14:256:16], T.sgm[:, 15:256:16], A.min)
-    do("v", V.tensor_scalar, ("mn", "jj"), "tj", T.tj[:, 0:15 * n + 1:n], T.mn[:], T.jj[:, 0:1], None, A.add)
-    do("v", V.tensor_tensor_scan, ("tj", "tjs", "rn"), "sj", T.sj[:, 0:16 * n], T.rn[:, 0:16 * n], T.tj[:, 0:16 * n], 0.0, A.mult, A.add)
-    do("v", V.tensor_copy, ("sj",), "fin", T.fin[:], T.sj[:, n - 1:16 * n:n])
+    do("v", V.tensor_copy, ("mn",), "fin", T.fin[:], T.mn[:])
 
     for b in (0, 1):
-        do("v", V.tensor_copy, ("dc", "own", "fin") + early, "t%d" % b, T.t2[:, 128 * b:128 * b + 128].bitcast(dt.uint32),
-           win[:].bitcast(dt.uint32).indirect(T.fin[:, 8 * b:8 * b + 8]))
-        act(("dsc", "own", "fin") + earlys, "t%ds" % b, T.t2s[:, 128 * b:128 * b + 128],
-            wins[:].indirect(T.fin[:, 8 * b:8 * b + 8]), F.Copy)
+        do("v", V.tensor_copy, ("dc", "loc", "fin"), "t%d" % b, T.t2[:, 128 * b:128 * b + 128].bitcast(dt.uint32),
+           T.win[:].bitcast(dt.uint32).indirect(T.fin[:, 8 * b:8 * b + 8]))
+        act(("dsc", "los", "fin"), "t%ds" % b, T.t2s[:, 128 * b:128 * b + 128],
+            T.wins[:].indirect(T.fin[:, 8 * b:8 * b + 8]), F.Copy)
     for b in (0, 1):
         for o in (0, 1):
             k = 2 * b + o
@@ -446,5 +376,4 @@ def rank_program(g, core, T, topo):
     for s, v in final.items():
         ev["end_" + s] = (s, v)
     ev["end_ls"] = ("ls", nls)
-    last = ["ls1", "m2", "dc", "dsc"] + list(early) + list(earlys)
-    need("g", *[k for k in ev if k.startswith("end_") or k.startswith("m1_")], *last)
+    need("g", *[k for k in ev if k.startswith("end_") or k.startswith("m1_")], "m2", "dc", "dsc")

@@ -14,18 +14,19 @@ SCRATCH = {}
 for _n, _w, _d in [
     ("one", 32, f32), ("onei", 8, i32),
     ("ct", 8, i32), ("tabf", 8, f32), ("tot", 32, f32), ("it8", 8, f32), ("offc", 8, u16),
-    ("fm", 272, f32), ("fa", 256, f32), ("dg", 256, f32), ("fm8", 40, f32), ("rst8", 40, f32),
+    ("fm", 144, f32), ("dg", 256, f32), ("fm8", 40, f32), ("rst8", 40, f32),
     ("i16", 8, f32), ("k8", 8, f32), ("ikh", 8, f32), ("ik2", 8, f32), ("idump", 40, f32), ("di", 40, f32),
-    ("pw", 8, f32), ("c5", 8, f32), ("kt5", 8, f32), ("thr", 8, f32),
-    ("bc", 128, f32), ("nrow", 128, f32), ("erow", 136, f32), ("nz", 128, f32), ("zrow", 128, f32),
+    ("pw", 8, f32), ("c5", 8, f32), ("c5h", 8, f32), ("kt5", 8, f32), ("thr", 8, f32),
+    ("bc", 128, bf), ("nrow", 128, bf), ("erow", 136, f32), ("nz", 128, bf), ("zrow", 128, bf),
     ("se", 128, f32), ("et", 12, f32), ("fl8", 8, f32), ("de", 8, f32), ("vv", 8, f32), ("pkf", 8, f32), ("pk", 4, u16),
-    ("junk", 1024, f32), ("acc", 8, f32), ("comp", 8, u16), ("ce", 128, f32), ("junl", 5 * C, f32), ("junp", 8, f32),
-    ("lfa", 12, f32), ("lsa", 12, u16), ("lfb", 12, f32), ("lsb", 12, u16), ("lfo", 6, f32), ("lso", 6, u16),
+    ("junk", 1024, f32), ("acc", 8, f32), ("comp", 8, u16), ("ce", 128, f32), ("nce", 2 * C, f32),
+    ("junl", 5 * C, f32), ("junp", 16, f32),
+    ("lsa", 12, u16), ("lfb", 12, f32), ("lsb", 12, u16), ("lfo", 6, f32), ("lso", 6, u16),
     ("l2", 20, u16), ("wi", 20, i32), ("dei", 40, i32), ("fli", 40, i32), ("def_", 40, f32), ("fd", 40, f32),
     ("prx", 40, f32), ("er", 40, f32), ("po", 40, f32), ("pos", 40, u16),
     ("slots", 5 * C, bf), ("mr2", TAB, bf), ("mk", 256, bf), ("g", 256, f32), ("sgm", 256, f32), ("mn", 16, f32),
     ("fin", 16, u16),
-    ("xb", 512, bf), ("xq", 128, c4), ("xs", 128, u8), ("xc", 128, c4), ("xcs", 128, u8),
+    ("xb", 512, bf), ("xq", 128, c4), ("xs", 128, u8), ("xc", C + DS, c4), ("xcs", C + DS, u8),
     ("spa", 2 * DS, c4), ("spas", 2 * DS, u8), ("spb", 2 * DS, c4), ("spbs", 2 * DS, u8),
     ("win", WIN, c4), ("wins", WIN, u8), ("t2", 256, c4), ("t2s", 256, u8),
     ("wb", 2048, bf), ("wq", 512, c4), ("ws", 512, u8), ("ysb", 512, f32),
@@ -35,7 +36,7 @@ for _n, _w, _d in [
 ONE = {k: i for i, k in enumerate(["paf", "paf5", "paf2", "pgf", "sg", "pa", "ia", "a0", "a1", "a2", "a3", "a4"])}
 ONEI = {k: i for i, k in enumerate(["ip", "ipa", "ipg"])}
 SCRATCH["ps"] = ("psum", [128, 2048], f32)
-SEMAPHORES = (["cl", "xl", "wl", "l2d", "vs", "ss", "ts", "gs", "ls", "m2", "dc", "dsc",
+SEMAPHORES = (["cl", "xl", "wl", "l2d", "pad", "vs", "ss", "ts", "gs", "ls", "m2", "dc", "dsc",
                "r1", "r2", "rc", "rsc", "st0"] + ["m1_%d" % s for s in range(N)])
 
 
@@ -183,29 +184,28 @@ def rank_program(g, core, T, topo):
 
     do("g", g.iota, (), "ip", onei["ip"], [[1, 1]], 0, 1)
     iota("it8", [[2, 4], [0, 2]])
-    iota("fm", [[0, 17], [1, 16]])
+    iota("fm", [[0, 9], [1, 16]])
     iota("er0", [[0, 1]], 0, T.erow[:, 7:8])
     iota("et0", [[0, 1]], 0, T.et[:, 0:1])
     iota("i16", [[16, 8]])
     iota("pw", [[0, 4], [256, 2]])
     iota("c5", [[P, 5]], (r - 2) * P - (N * P if up else 0), T.c5[:, 0:5])
-    for k in range(n):
-        do("v", V.memset, (), "slots", T.slots[:, C * k:C * k + C], float(OFF + DS * k))
     do("v", V.tensor_scalar, ("ip",), "ipa", onei["ipa"], onei["ip"], 15, None, A.bitwise_and)
     do("v", V.tensor_scalar, ("ip",), "ipg", onei["ipg"], onei["ip"], 4, 1, A.logical_shift_right, A.bitwise_and)
     do("v", V.tensor_copy, ("ipa",), "paf", paf, onei["ipa"])
     do("v", V.tensor_copy, ("ipg",), "pgf", one["pgf"], onei["ipg"])
     do("v", V.tensor_scalar, ("it8", "pgf"), "offc", T.offc[:], T.it8[:], one["pgf"], None, A.add)
-    do("v", V.memset, (), "mr0", T.mr2[:, SH:SH + P], 0.0)
+    do("v", V.tensor_scalar, ("fm", "paf"), "dg", T.dg[:, 0:128], T.fm[:, 1:129], paf, BIG, A.is_equal, A.mult)
     act(("paf",), "paf5", one["paf5"], paf, bias=0.5)
     act(("i16", "paf5"), "k8", T.k8[:], T.i16[:], bias=one["paf5"])
-    act(("fm", "paf"), "fa", T.fa[:], T.fm[:, 1:257], F.Abs, bias=paf, scale=-1.0)
-    act(("fa",), "dg", T.dg[:], T.fa[:], F.Relu, bias=BIG, scale=-BIG)
+    act(("c5",), "c5h", T.c5h[:, 0:5], T.c5[:, 0:5], bias=0.5)
 
     end = T.erow[:, 8:136]
     mine = T.erow[:, 135:136]
     do("v", V.tensor_copy, ("ct", "offc"), "bc", T.bc[:], T.ct[:, 0:8].indirect(T.offc[:]))
+    do("v", V.tensor_copy, ("ct",), "tabf", T.tabf[:], T.ct[:])
     do("v", V.transpose, ("bc",), "nrow", T.nrow[:], T.bc[:])
+    act(("tabf",), "fl8", T.fl8[:], T.tabf[:], F.Relu, scale=-128.0, bias=128.0)
     act(("nrow",), "nz", T.nz[:], T.nrow[:], F.Sign)
     do("v", V.tensor_tensor_scan, ("nrow",), "erow", end, T.nrow[:], T.nrow[:], 0.0, A.add, A.max)
 
@@ -221,8 +221,11 @@ def rank_program(g, core, T, topo):
 
     do("v", V.tensor_tensor_scan, ("erow", "er0", "dg"), "se", T.se[:], T.erow[:, 7:135], T.dg[:, 0:128], BIG, A.min, A.max)
     do("v", V.tensor_tensor_scan, ("nz",), "zrow", T.zrow[:], T.nz[:], T.nz[:], 0.0, A.add, A.max)
-    do("v", V.tensor_copy, ("ct",), "tabf", T.tabf[:], T.ct[:])
-    act(("tabf",), "fl8", T.fl8[:], T.tabf[:], F.Relu, scale=-128.0, bias=128.0)
+    act(("erow",), "tot", T.tot[:, 4 * r:4 * r + 1], mine, F.Copy)
+    kt, ktk = T.c5h, "c5h"
+    if up:
+        act(("c5h", "erow"), "kt5", T.kt5[:, 0:5], T.c5h[:, 0:5], bias=mine)
+        kt, ktk = T.kt5, "kt5"
     for c in range(8):
         act(("zrow", "k8"), "acc", T.junk[:, 128 * c:128 * c + 127], T.zrow[:, 0:127], F.Sign,
             bias=T.k8[:, c:c + 1], scale=-1.0, accum_out=T.acc[:, c:c + 1])
@@ -240,27 +243,33 @@ def rank_program(g, core, T, topo):
     dma("y", ("pk",), "l2own", "l2d", T.l2[:, o:o + 4], T.pk[:])
 
     do("v", V.quantize_mx, ("xb",), "xq", T.xq[:], T.xs[:], T.xb[:])
+    do("v", V.memset, (), "mr0", T.mr2[:, SH:SH + P], 0.0)
+    do("v", V.tensor_scalar, ("fm", "paf"), "dg2", T.dg[:, 128:256], T.fm[:, 1:129], paf, BIG, A.is_equal, A.mult)
     do("v", V.tensor_scalar, ("acc",), "comp", T.comp[:], T.acc[:], 0.5, 63.5, A.mult, A.add)
-    do("v", V.tensor_copy, ("xq", "comp"), "xc", T.xc[:].bitcast(dt.uint32), T.xq[:].bitcast(dt.uint32).indirect(T.comp[:, 0:8]))
+    for k in range(2):
+        do("v", V.memset, (), "slots", T.slots[:, C * k:C * k + C], float(OFF + DS * k))
+    do("v", V.tensor_copy, ("xq", "comp"), "xc", T.xc[:, 0:C].bitcast(dt.uint32), T.xq[:].bitcast(dt.uint32).indirect(T.comp[:, 0:8]))
     act(("erow", "comp"), "ce", T.ce[:], end.indirect(T.comp[:, 0:8]), F.Copy)
-    act(("erow",), "tot", T.tot[:, 4 * r:4 * r + 1], mine, F.Copy)
-    act(("xq", "comp"), "xcs", T.xcs[:], T.xs[:].indirect(T.comp[:, 0:8]), F.Copy)
+    act(("xq", "comp"), "xcs", T.xcs[:, 0:C], T.xs[:].indirect(T.comp[:, 0:8]), F.Copy)
+    for k in range(2, n):
+        do("v", V.memset, (), "slots", T.slots[:, C * k:C * k + C], float(OFF + DS * k))
     do("v", V.quantize_mx, ("wb",), "wq", T.wq[:], T.ws[:], T.wb[:])
+    dma("y", ("xq",), "xpad", "pad", codes(T.xc[:, C:C + DS]), codes(T.xq[:, 0:DS]))
+    dma("y", ("xq",), "xpad", "pad", T.xcs[:, C:C + DS], T.xs[:, 0:DS])
 
     iota("ikh", [[16, 8]])
     iota("prz", [[0, 40]], 0, T.prx[:])
-    iota("idump", [[16, 40]], DUMP)
-    iota("fm8", [[0, 5], [1, 8]])
     if r < 3:
         iota("pr0", [[0, 1]], SH - r * P, T.prx[:, 0:1], reads=("prz",))
+    iota("fm8", [[0, 5], [1, 8]])
+    iota("idump", [[16, 40]], DUMP)
     act(("paf",), "paf2", one["paf2"], paf, scale=2.0, bias=127.0)
     act(("ikh", "paf2"), "ik2", T.ik2[:], T.ikh[:], scale=2.0, bias=one["paf2"])
-    act(("idump", "paf"), "di", T.di[:], T.idump[:], bias=paf)
+    for i, q in enumerate(hop):
+        d = q - (r - 2)
+        act(("ce", ktk), "nce", T.nce[:, C * i:C * i + 127], T.ce[:, 0:127], scale=-1.0, bias=kt[:, d:d + 1])
     act(("fm8",), "rst8", T.rst8[:], T.fm8[:], F.Sign)
-    kt, ktk = T.c5[:, 0:5], "c5"
-    if up:
-        act(("c5", "erow"), "kt5", T.kt5[:, 0:5], T.c5[:, 0:5], bias=mine)
-        kt, ktk = T.kt5[:, 0:5], "kt5"
+    act(("idump", "paf"), "di", T.di[:], T.idump[:], bias=paf)
 
     n2, nd = 0, 0
     for s in range(N):
@@ -276,15 +285,9 @@ def rank_program(g, core, T, topo):
     ev["m2"], ev["dc"], ev["dsc"] = ("m2", n2), ("dc", nd), ("dsc", nd)
 
     ns = needs(r)
-    keys = ["m1_%d" % s for s in ns]
-    if not ns:
-        do("v", V.tensor_scalar, (ktk,), "thr", T.thr[:, 0:5], kt, 0.5, None, A.add)
-    else:
-        sg = T.tot[:, 4 * ns[0]:4 * ns[0] + 1]
-        if len(ns) > 1:
-            do("v", V.tensor_reduce, keys, "sg", one["sg"], T.tot[:, 4 * ns[0]:4 * ns[-1] + 1:4], X, A.add)
-            sg, keys = one["sg"], ["sg"]
-        do("v", V.tensor_scalar, [ktk] + keys, "thr", T.thr[:, 0:5], kt, sg, 0.5, A.add if up else A.subtract, A.add)
+    if ns:
+        act(["m1_%d" % s for s in ns], "sg", T.junp[:, 8:8 + len(ns)], T.tot[:, 4 * ns[0]:4 * ns[-1] + 1:4], F.Copy,
+            scale=1.0 if up else -1.0, accum_out=one["sg"])
 
     if r == 3:
         do("v", V.tensor_scalar, ("prz", "m1_0"), "pr0", T.prx[:, 0:1], T.tot[:, 0:1], float(SH - r * P), None, A.add)
@@ -296,11 +299,25 @@ def rank_program(g, core, T, topo):
     do("v", V.tensor_tensor_scan, ["m1_%d" % s for s in range(fi, hi) if s != r] + ["tot", "pr0", "prz"], "prx",
        T.prx[:, 8:8 * (n - 1) + 1:8], steps, steps, T.prx[:, 0:1], A.add, A.max)
 
-    def lists(dsts, lf, ls, name):
-        for i, q in enumerate(dsts):
+    for i, q in enumerate(hop):
+        d = q - (r - 2)
+        row = T.nce[:, C * i:C * i + 127]
+        if ns:
+            act(("nce", "sg"), "a%d" % d, T.junl[:, C * d:C * d + 127], row, F.Sign, bias=one["sg"], accum_out=one["a%d" % d])
+        else:
+            act(("nce",), "a%d" % d, T.junl[:, C * d:C * d + 127], row, F.Sign, accum_out=one["a%d" % d])
+    thr, tk = kt, ktk
+    if ns:
+        act((ktk, "sg"), "thr", T.thr[:, 0:5], kt[:, 0:5], bias=one["sg"])
+        thr, tk = T.thr, "thr"
+
+    def counts(dsts):
+        for q in dsts:
             d = q - (r - 2)
-            act(("ce", "thr"), "a%d" % d, T.junl[:, C * d:C * d + 127], T.ce[:, 0:127], F.Sign,
-                bias=T.thr[:, d:d + 1], scale=-1.0, accum_out=one["a%d" % d])
+            act(("ce", tk), "a%d" % d, T.junl[:, C * d:C * d + 127], T.ce[:, 0:127], F.Sign,
+                bias=thr[:, d:d + 1], scale=-1.0, accum_out=one["a%d" % d])
+
+    def lists(dsts, lf, name):
         for i, q in enumerate(dsts):
             d = q - (r - 2)
             act(("ik2", "a%d" % d), name + "f", lf[:, 5 * i:5 * i + 5], T.ik2[:, 0:5], bias=one["a%d" % d])
@@ -308,28 +325,29 @@ def rank_program(g, core, T, topo):
     def clamp(k, lf, ls, name):
         do("v", V.tensor_scalar, (name + "f",), name, ls[:, 0:5 * k], lf[:, 0:5 * k], 0.5, 127.0, A.mult, A.min)
 
-    def pick(k, dst, dsts, ls, name):
-        do("v", V.tensor_copy, ("xc", name), name + "c", dst.bitcast(dt.uint32), T.xc[:].bitcast(dt.uint32).indirect(ls[:, 0:5 * k]))
-        act(("xcs", name), name + "s", dsts, T.xcs[:].indirect(ls[:, 0:5 * k]), F.Copy)
+    def pick(k, dst, ls, name, *keys):
+        do("v", V.tensor_copy, ("xc", name) + keys, name + "c", dst.bitcast(dt.uint32),
+           T.xc[:, 0:C + DS * len(keys)].bitcast(dt.uint32).indirect(ls[:, 0:5 * k]))
+
+    def picks(k, dst, ls, name, *keys):
+        act(("xcs", name) + keys, name + "s", dst, T.xcs[:, 0:C + DS * len(keys)].indirect(ls[:, 0:5 * k]), F.Copy)
     ka, kb = len(hop), len(dr)
-    lists(hop, T.lfa, T.lsa, "la")
-    clamp(ka, T.lfa, T.lsa, "la")
-    pick(ka, T.spa[:, 0:DS * ka], T.spas[:, 0:DS * ka], T.lsa, "la")
+    counts(dr[:1])
+    for i, q in enumerate(hop):
+        a = "a%d" % (q - (r - 2))
+        do("v", V.tensor_scalar, ("ik2", a), "la", T.lsa[:, 5 * i:5 * i + 5], T.ik2[:, 0:5], one[a], 0.5, A.add, A.mult)
+    pick(ka, T.spa[:, 0:DS * ka], T.lsa, "la", "xpad")
+    picks(ka, T.spas[:, 0:DS * ka], T.lsa, "la", "xpad")
     relay = [(me["X"], chip), (me["Y"], chipy)]
     need("g", "lac")
     nls += send([(c, es, codes(T.rcb[:]), codes(T.spa[:, DS * i:DS * i + DS])) for i, (c, es) in enumerate(relay[:ka])], "rc")
     need("g", "las")
     nls += send([(c, es, T.rsb[:], T.spas[:, DS * i:DS * i + DS]) for i, (c, es) in enumerate(relay[:ka])], "rsc")
-    lists(dr, T.lfb, T.lsb, "lb")
-    clamp(kb, T.lfb, T.lsb, "lb")
-    pick(kb, T.spb[:, 0:DS * kb], T.spbs[:, 0:DS * kb], T.lsb, "lb")
-    need("g", "lbc")
-    nls += send([(T.cores[q], direct_engines(i), codes(T.win[:, base(r, q):base(r, q) + DS]), codes(T.spb[:, DS * i:DS * i + DS]))
-                 for i, q in enumerate(dr)], "dc")
-    need("g", "lbs")
-    nls += send([(T.cores[q], direct_engines(i), T.wins[:, base(r, q):base(r, q) + DS], T.spbs[:, DS * i:DS * i + DS])
-                 for i, q in enumerate(dr)], "dsc")
-    lists([r], T.lfo, T.lso, "lo")
+    counts(dr[1:])
+    lists(dr, T.lfb, "lb")
+    counts([r])
+    lists([r], T.lfo, "lo")
+    act(("prx",), "ia", T.junp[:, 0:n - 1], T.prx[:, 8:8 * (n - 1) + 1:8], F.Sign, scale=-1.0, bias=SH + 0.5, accum_out=one["ia"])
 
     do("v", V.tensor_copy, ("m2", "l2own"), "wi", T.wi[:, 0:4 * n], T.l2[:, 0:4 * n])
     wi = T.wi[:, 0:4 * n]
@@ -339,19 +357,28 @@ def rank_program(g, core, T, topo):
     do("v", V.tensor_scalar, ("wi",), "fli2", T.fli[:, 0:m:2], wi, 15, None, A.logical_shift_right)
     do("v", V.tensor_tensor, ("dei2", "prx"), "def_", T.def_[:, 0:m], T.dei[:, 0:m], T.prx[:, 0:m], A.add)
     do("v", V.tensor_tensor, ("fli2", "di"), "fd", T.fd[:, 0:m], T.fli[:, 0:m], T.di[:, 0:m], A.mult)
+    clamp(kb, T.lfb, T.lsb, "lb")
     do("v", V.tensor_tensor_scan, ("def_", "rst8"), "er", T.er[:, 0:m], T.rst8[:, 0:m], T.def_[:, 0:m], 0.0, A.mult, A.add)
-    clamp(1, T.lfo, T.lso, "lo")
+    pick(kb, T.spb[:, 0:DS * kb], T.lsb, "lb")
+    picks(kb, T.spbs[:, 0:DS * kb], T.lsb, "lb")
+    need("g", "lbc")
+    nls += send([(T.cores[q], direct_engines(i), codes(T.win[:, base(r, q):base(r, q) + DS]), codes(T.spb[:, DS * i:DS * i + DS]))
+                 for i, q in enumerate(dr)], "dc")
+    need("g", "lbs")
+    nls += send([(T.cores[q], direct_engines(i), T.wins[:, base(r, q):base(r, q) + DS], T.spbs[:, DS * i:DS * i + DS])
+                 for i, q in enumerate(dr)], "dsc")
     do("v", V.tensor_tensor, ("er", "fd"), "po", T.po[:, 0:m], T.er[:, 0:m], T.fd[:, 0:m], A.add)
-    b = base(r, r)
-    pick(1, T.win[:, b:b + DS], T.wins[:, b:b + DS], T.lso, "lo")
+    clamp(1, T.lfo, T.lso, "lo")
     do("v", V.tensor_copy, ("po",), "pos", T.pos[:, 0:m], T.po[:, 0:m])
-    act(("prx",), "ia", T.junp[:, 0:n - 1], T.prx[:, 8:8 * (n - 1) + 1:8], F.Sign, scale=-1.0, bias=SH + 0.5, accum_out=one["ia"])
     act(("ia",), "g0", T.g[:, 0:1], one["ia"], scale=DS / 2.0, bias=float(OFF + DS * (n - 1) // 2))
 
     do("v", V.tensor_copy, ("pos", "slots", "mr0"), "mr2", T.mr2[:].indirect(T.pos[:, 0:m]), T.slots[:, 0:16 * m])
+    b = base(r, r)
+    pick(1, T.win[:, b:b + DS], T.lso, "lo")
+    picks(1, T.wins[:, b:b + DS], T.lso, "lo")
     do("v", V.tensor_scalar, ("mr2",), "mk", T.mk[:], T.mr2[:, SH:SH + P], 0.0, None, A.is_gt)
     do("v", V.tensor_tensor_scan, ("mk", "g0"), "g", T.g[:, 1:P], T.mk[:, 1:P], T.mr2[:, SH + 1:SH + P], T.g[:, 0:1], A.add, A.max)
-    do("v", V.tensor_tensor_scan, ("g", "dg"), "sgm", T.sgm[:], T.g[:], T.dg[:], BIG, A.min, A.max)
+    do("v", V.tensor_tensor_scan, ("g", "dg2"), "sgm", T.sgm[:], T.g[:], T.dg[:], BIG, A.min, A.max)
     do("v", V.tensor_tensor, ("sgm",), "mn", T.mn[:], T.sgm[:, 14:256:16], T.sgm[:, 15:256:16], A.min)
     do("v", V.tensor_copy, ("mn",), "fin", T.fin[:], T.mn[:])
 

from concourse.bass import DstId, RemoteDMATransfer
from concourse.mybir import dt, AluOpType as A, AxisListType, ActivationFunctionType as F

N, C, P, DS = 8, 128, 256, 80
OFF = 16
WIN = OFF + 5 * DS
SH = 2048
DUMP = 4112
TAB = DUMP + 4096 + 5 * C + 16
BIG = 1.0e6

f32, bf, i32, u16, u8, c4 = "float32", "bfloat16", "int32", "uint16", "uint8", "float8_e4m3fn_x4"
SCRATCH = {}
for _n, _w, _d in [
    ("one", 32, f32), ("onei", 8, i32),
    ("ct", 8, i32), ("tabf", 8, f32), ("tot", 32, f32), ("it8", 8, f32), ("offc", 8, u16),
    ("fm", 144, f32), ("dg", 256, f32), ("fm8", 40, f32), ("rst8", 40, f32),
    ("i16", 8, f32), ("k8", 8, f32), ("ikh", 8, f32), ("ik2", 8, f32), ("idump", 40, f32), ("di", 40, f32),
    ("pw", 8, f32), ("c5", 8, f32), ("c5h", 8, f32), ("kt5", 8, f32), ("thr", 8, f32),
    ("bc", 128, bf), ("nrow", 128, bf), ("erow", 136, f32), ("nz", 128, bf), ("zrow", 128, bf),
    ("se", 128, f32), ("et", 12, f32), ("fl8", 8, f32), ("de", 8, f32), ("vv", 8, f32), ("pkf", 8, f32), ("pk", 4, u16),
    ("junk", 1024, f32), ("acc", 8, f32), ("comp", 8, u16), ("ce", 128, f32), ("nce", 2 * C, f32),
    ("junl", 5 * C, f32), ("junp", 16, f32),
    ("lsa", 12, u16), ("lfb", 12, f32), ("lsb", 12, u16), ("lfo", 6, f32), ("lso", 6, u16),
    ("l2", 20, u16), ("wi", 20, i32), ("dei", 40, i32), ("fli", 40, i32), ("def_", 40, f32), ("fd", 40, f32),
    ("prx", 40, f32), ("er", 40, f32), ("po", 40, f32), ("pos", 40, u16),
    ("slots", 5 * C, bf), ("mr2", TAB, bf), ("mk", 256, bf), ("g", 256, f32), ("sgm", 256, f32), ("mn", 16, f32),
    ("fin", 16, u16),
    ("xb", 512, bf), ("xq", 128, c4), ("xs", 128, u8), ("xc", C + DS, c4), ("xcs", C + DS, u8),
    ("spa", 2 * DS, c4), ("spas", 2 * DS, u8), ("spb", 2 * DS, c4), ("spbs", 2 * DS, u8),
    ("win", WIN, c4), ("wins", WIN, u8), ("t2", 256, c4), ("t2s", 256, u8),
    ("wb", 2048, bf), ("wq", 512, c4), ("ws", 512, u8), ("ysb", 512, f32),
    ("r1b", 1, f32), ("r2b", 4, u16), ("rcb", DS, c4), ("rsb", DS, u8),
]:
    SCRATCH[_n] = ("sbuf", [128, _w], _d)
ONE = {k: i for i, k in enumerate(["paf", "paf5", "paf2", "pgf", "sg", "pa", "ia", "a0", "a1", "a2", "a3", "a4"])}
ONEI = {k: i for i, k in enumerate(["ip", "ipa", "ipg"])}
SCRATCH["ps"] = ("psum", [128, 2048], f32)
SEMAPHORES = (["cl", "xl", "wl", "l2d", "pad", "vs", "ss", "ts", "gs", "ls", "m2", "dc", "dsc",
               "r1", "r2", "rc", "rsc", "st0"] + ["m1_%d" % s for s in range(N)])


def needs(q):
    return list(range(q)) if q < N // 2 else list(range(q + 1, N))


def first(q):
    return max(0, q - 2)


def base(s, q):
    return OFF + DS * (s - first(q))


def plan(T, topo):
    out = []
    for r in range(N):
        core = T.cores[r]
        near = [q for q in (r - 1, r + 1, r - 2, r + 2) if 0 <= q < N]
        far = [q for q in range(N) if q not in near and q != r and r in needs(q)]
        direct = [q for q in near if topo.may_write(core, T.cores[q])]
        hop = [q for q in near if q not in direct]
        relays = [c for c in topo.cores_of(core) if c != core and all(topo.may_write(c, T.cores[q]) for q in hop + far)]
        X = [c for c in relays if topo.die(c) == topo.die(core)][0]
        Y = [c for c in relays if topo.die(c) != topo.die(core)][0]
        out.append({"direct": direct, "hop": hop, "hop1": hop + far, "X": X, "Y": Y})
    return out


def mask_of(es):
    return sum(1 << e for e in es)


def part(es, k, n):
    w = len(es) // n
    return es[k * w:k * w + w]


def sender(g, core, T, topo):
    def send(items, rsem):
        tr = []
        for dst, es, o, i in items:
            rid, pid = topo.addr(dst, core)
            tr.append(RemoteDMATransfer(dst_ids=[DstId(rid=rid, pnc=pid)], dma_engine_mask=mask_of(es),
                                        remote_sem=T.sem[rsem], src=i, dst=o))
        g.remote_dma_fused(tr, local_sem=T.sem["ls"])
        return sum(len(es) for _, es, _, _ in items)
    return send


def codes(v):
    return v.bitcast(dt.uint8)


def relay_program(g, core, T, topo, pl, r, isx):
    me = pl[r]
    send = sender(g, core, T, topo)
    n = 0
    dsts = me["hop1"] if isx else me["hop"]
    g.wait_ge(T.sem["r1" if isx else "r2"], 8)
    it = []
    for k, q in enumerate(dsts):
        dst = T.cores[q]
        es = part(topo.engines(core, dst), k, len(dsts))
        if isx:
            it.append((dst, es, T.tot[:, 4 * r:4 * r + 1], T.r1b[:]))
        else:
            o = 4 * (r - first(q))
            it.append((dst, es, T.l2[:, o:o + 4], T.r2b[:]))
    n += send(it, "m1_%d" % r if isx else "m2")
    for k, q in enumerate(me["hop"]):
        if (k == 0) == isx:
            dst = T.cores[q]
            es = topo.engines(core, dst)
            b = base(r, q)
            g.wait_ge(T.sem["rc"], 8)
            n += send([(dst, es, codes(T.win[:, b:b + DS]), codes(T.rcb[:]))], "dc")
            g.wait_ge(T.sem["rsc"], 8)
            n += send([(dst, es, T.wins[:, b:b + DS], T.rsb[:])], "dsc")
    g.wait_ge(T.sem["ls"], n)


def rank_program(g, core, T, topo):
    pl = plan(T, topo)
    r = T.rank_of(core)
    if r is None:
        for k in range(N):
            if core == pl[k]["X"]:
                relay_program(g, core, T, topo, pl, k, True)
            if core == pl[k]["Y"]:
                relay_program(g, core, T, topo, pl, k, False)
        return
    me = pl[r]
    send = sender(g, core, T, topo)
    queues = {"v": g.vector, "s": g.scalar, "t": g.tensor, "g": g, "y": g.sync}
    own = {"v": "vs", "s": "ss", "t": "ts", "g": "gs"}
    count = {"v": 0, "s": 0, "t": 0, "g": 0}
    ev, seen, final = {}, {}, {}

    def need(q, *keys):
        m = {}
        for k in keys:
            s, v = ev[k]
            m[s] = max(m.get(s, 0), v)
        for s, v in m.items():
            if seen.get((q, s), 0) < v:
                queues[q].wait_ge(T.sem[s], v)
                seen[(q, s)] = v

    def do(q, fn, reads, write, *a, **kw):
        need(q, *reads)
        fn(*a, **kw).then_inc(T.sem[own[q]], 1)
        count[q] += 1
        ev[write] = (own[q], count[q])

    def dma(q, reads, write, sem, out, in_):
        need(q, *reads)
        queues[q].dma_start(out, in_).then_inc(T.sem[sem], 16)
        final[sem] = final.get(sem, 0) + 16
        ev[write] = (sem, final[sem])

    V, S = g.vector, g.scalar
    X = AxisListType.X
    one = {k: T.one[:, i:i + 1] for k, i in ONE.items()}
    onei = {k: T.onei[:, i:i + 1] for k, i in ONEI.items()}
    paf = one["paf"]
    up = r >= N // 2
    fi, hi = first(r), min(N - 1, r + 2)
    n = hi - fi + 1
    m = 8 * n

    def iota(name, pattern, base_=0, out=None, reads=()):
        do("g", g.iota, reads, name, T[name][:] if out is None else out, pattern, base_, 0,
           allow_small_or_imprecise_dtypes=True)

    def act(reads, write, out, in_, func=F.Identity, **kw):
        do("s", S.activation, reads, write, out, in_, func, **kw)

    for k in range(4):
        for q, j in (("y", 2 * k), ("s", 2 * k + 1)):
            dma(q, (), "ct", "cl", T.ct[16 * j:16 * j + 16, 0:8], T.cnt[:])
    dma("y", (), "xb", "xl", T.xb[:], T.x[:])
    dma("y", (), "wb", "wl", T.wb[:], T.w[:])

    do("g", g.iota, (), "ip", onei["ip"], [[1, 1]], 0, 1)
    iota("it8", [[2, 4], [0, 2]])
    iota("fm", [[0, 9], [1, 16]])
    iota("er0", [[0, 1]], 0, T.erow[:, 7:8])
    iota("et0", [[0, 1]], 0, T.et[:, 0:1])
    iota("i16", [[16, 8]])
    iota("pw", [[0, 4], [256, 2]])
    iota("c5", [[P, 5]], (r - 2) * P - (N * P if up else 0), T.c5[:, 0:5])
    do("v", V.tensor_scalar, ("ip",), "ipa", onei["ipa"], onei["ip"], 15, None, A.bitwise_and)
    do("v", V.tensor_scalar, ("ip",), "ipg", onei["ipg"], onei["ip"], 4, 1, A.logical_shift_right, A.bitwise_and)
    do("v", V.tensor_copy, ("ipa",), "paf", paf, onei["ipa"])
    do("v", V.tensor_copy, ("ipg",), "pgf", one["pgf"], onei["ipg"])
    do("v", V.tensor_scalar, ("it8", "pgf"), "offc", T.offc[:], T.it8[:], one["pgf"], None, A.add)
    do("v", V.tensor_scalar, ("fm", "paf"), "dg", T.dg[:, 0:128], T.fm[:, 1:129], paf, BIG, A.is_equal, A.mult)
    act(("paf",), "paf5", one["paf5"], paf, bias=0.5)
    act(("i16", "paf5"), "k8", T.k8[:], T.i16[:], bias=one["paf5"])
    act(("c5",), "c5h", T.c5h[:, 0:5], T.c5[:, 0:5], bias=0.5)

    end = T.erow[:, 8:136]
    mine = T.erow[:, 135:136]
    do("v", V.tensor_copy, ("ct", "offc"), "bc", T.bc[:], T.ct[:, 0:8].indirect(T.offc[:]))
    do("v", V.tensor_copy, ("ct",), "tabf", T.tabf[:], T.ct[:])
    do("v", V.transpose, ("bc",), "nrow", T.nrow[:], T.bc[:])
    act(("tabf",), "fl8", T.fl8[:], T.tabf[:], F.Relu, scale=-128.0, bias=128.0)
    act(("nrow",), "nz", T.nz[:], T.nrow[:], F.Sign)
    do("v", V.tensor_tensor_scan, ("nrow",), "erow", end, T.nrow[:], T.nrow[:], 0.0, A.add, A.max)

    nls = 0
    need("g", "erow")
    chip, chipy = part(topo.engines(core, me["X"]), 0, 2), part(topo.engines(core, me["Y"]), 1, 2)
    dr, hop = me["direct"], me["hop"]

    def direct_engines(k):
        return part(topo.engines(core, T.cores[dr[k]]), k, len(dr))
    nls += send([(me["X"], chip, T.r1b[:], mine)], "r1")
    nls += send([(T.cores[q], direct_engines(k), T.tot[:, 4 * r:4 * r + 1], mine) for k, q in enumerate(dr)], "m1_%d" % r)

    do("v", V.tensor_tensor_scan, ("erow", "er0", "dg"), "se", T.se[:], T.erow[:, 7:135], T.dg[:, 0:128], BIG, A.min, A.max)
    do("v", V.tensor_tensor_scan, ("nz",), "zrow", T.zrow[:], T.nz[:], T.nz[:], 0.0, A.add, A.max)
    act(("erow",), "tot", T.tot[:, 4 * r:4 * r + 1], mine, F.Copy)
    kt, ktk = T.c5h, "c5h"
    if up:
        act(("c5h", "erow"), "kt5", T.kt5[:, 0:5], T.c5h[:, 0:5], bias=mine)
        kt, ktk = T.kt5, "kt5"
    for c in range(8):
        act(("zrow", "k8"), "acc", T.junk[:, 128 * c:128 * c + 127], T.zrow[:, 0:127], F.Sign,
            bias=T.k8[:, c:c + 1], scale=-1.0, accum_out=T.acc[:, c:c + 1])
    do("v", V.tensor_tensor, ("se",), "et", T.et[:, 1:9], T.se[:, 14:128:16], T.se[:, 15:128:16], A.min)
    do("v", V.tensor_tensor, ("et", "et0"), "de", T.de[:], T.et[:, 1:9], T.et[:, 0:8], A.subtract)
    do("v", V.tensor_tensor, ("de", "fl8"), "vv", T.vv[:], T.de[:], T.fl8[:], A.add)
    do("v", V.tensor_tensor_scan, ("vv", "pw"), "pkf", T.pkf[:], T.pw[:], T.vv[:], 0.0, A.mult, A.add)
    do("v", V.tensor_copy, ("pkf",), "pk", T.pk[:], T.pkf[:, 1:8:2])

    need("g", "pk")
    nls += send([(me["Y"], chipy, T.r2b[:], T.pk[:])], "r2")
    nls += send([(T.cores[q], direct_engines(k), T.l2[:, 4 * (r - first(q)):4 * (r - first(q)) + 4], T.pk[:])
                 for k, q in enumerate(dr)], "m2")
    o = 4 * (r - fi)
    dma("y", ("pk",), "l2own", "l2d", T.l2[:, o:o + 4], T.pk[:])

    do("v", V.quantize_mx, ("xb",), "xq", T.xq[:], T.xs[:], T.xb[:])
    do("v", V.memset, (), "mr0", T.mr2[:, SH:SH + P], 0.0)
    do("v", V.tensor_scalar, ("fm", "paf"), "dg2", T.dg[:, 128:256], T.fm[:, 1:129], paf, BIG, A.is_equal, A.mult)
    do("v", V.tensor_scalar, ("acc",), "comp", T.comp[:], T.acc[:], 0.5, 63.5, A.mult, A.add)
    for k in range(2):
        do("v", V.memset, (), "slots", T.slots[:, C * k:C * k + C], float(OFF + DS * k))
    do("v", V.tensor_copy, ("xq", "comp"), "xc", T.xc[:, 0:C].bitcast(dt.uint32), T.xq[:].bitcast(dt.uint32).indirect(T.comp[:, 0:8]))
    act(("erow", "comp"), "ce", T.ce[:], end.indirect(T.comp[:, 0:8]), F.Copy)
    act(("xq", "comp"), "xcs", T.xcs[:, 0:C], T.xs[:].indirect(T.comp[:, 0:8]), F.Copy)
    for k in range(2, n):
        do("v", V.memset, (), "slots", T.slots[:, C * k:C * k + C], float(OFF + DS * k))
    do("v", V.quantize_mx, ("wb",), "wq", T.wq[:], T.ws[:], T.wb[:])
    dma("y", ("xq",), "xpad", "pad", codes(T.xc[:, C:C + DS]), codes(T.xq[:, 0:DS]))
    dma("y", ("xq",), "xpad", "pad", T.xcs[:, C:C + DS], T.xs[:, 0:DS])

    iota("ikh", [[16, 8]])
    iota("prz", [[0, 40]], 0, T.prx[:])
    if r < 3:
        iota("pr0", [[0, 1]], SH - r * P, T.prx[:, 0:1], reads=("prz",))
    iota("fm8", [[0, 5], [1, 8]])
    iota("idump", [[16, 40]], DUMP)
    act(("paf",), "paf2", one["paf2"], paf, scale=2.0, bias=127.0)
    act(("ikh", "paf2"), "ik2", T.ik2[:], T.ikh[:], scale=2.0, bias=one["paf2"])
    for i, q in enumerate(hop):
        d = q - (r - 2)
        act(("ce", ktk), "nce", T.nce[:, C * i:C * i + 127], T.ce[:, 0:127], scale=-1.0, bias=kt[:, d:d + 1])
    act(("fm8",), "rst8", T.rst8[:], T.fm8[:], F.Sign)
    act(("idump", "paf"), "di", T.di[:], T.idump[:], bias=paf)

    n2, nd = 0, 0
    for s in range(N):
        for kind in ("hop1", "direct"):
            if r in pl[s][kind]:
                ev["m1_%d" % s] = ("m1_%d" % s, 8 // len(pl[s][kind]))
        if r in pl[s]["hop"]:
            n2 += 8 // len(pl[s]["hop"])
            nd += 8
        elif r in pl[s]["direct"]:
            n2 += 8 // len(pl[s]["direct"])
            nd += 8 // len(pl[s]["direct"])
    ev["m2"], ev["dc"], ev["dsc"] = ("m2", n2), ("dc", nd), ("dsc", nd)

    ns = needs(r)
    if ns:
        act(["m1_%d" % s for s in ns], "sg", T.junp[:, 8:8 + len(ns)], T.tot[:, 4 * ns[0]:4 * ns[-1] + 1:4], F.Copy,
            scale=1.0 if up else -1.0, accum_out=one["sg"])

    if r == 3:
        do("v", V.tensor_scalar, ("prz", "m1_0"), "pr0", T.prx[:, 0:1], T.tot[:, 0:1], float(SH - r * P), None, A.add)
    elif up:
        do("v", V.tensor_reduce, ["m1_%d" % s for s in range(fi, N) if s != r] + ["tot"], "pa", one["pa"],
           T.tot[:, 4 * fi:4 * (N - 1) + 1:4], X, A.add)
        do("v", V.tensor_scalar, ("prz", "pa"), "pr0", T.prx[:, 0:1], one["pa"], -1.0, float(SH + (N - r) * P), A.mult, A.add)
    steps = T.tot[:, 4 * fi:4 * (hi - 1) + 1:4]
    do("v", V.tensor_tensor_scan, ["m1_%d" % s for s in range(fi, hi) if s != r] + ["tot", "pr0", "prz"], "prx",
       T.prx[:, 8:8 * (n - 1) + 1:8], steps, steps, T.prx[:, 0:1], A.add, A.max)

    for i, q in enumerate(hop):
        d = q - (r - 2)
        row = T.nce[:, C * i:C * i + 127]
        if ns:
            act(("nce", "sg"), "a%d" % d, T.junl[:, C * d:C * d + 127], row, F.Sign, bias=one["sg"], accum_out=one["a%d" % d])
        else:
            act(("nce",), "a%d" % d, T.junl[:, C * d:C * d + 127], row, F.Sign, accum_out=one["a%d" % d])
    thr, tk = kt, ktk
    if ns:
        act((ktk, "sg"), "thr", T.thr[:, 0:5], kt[:, 0:5], bias=one["sg"])
        thr, tk = T.thr, "thr"

    def counts(dsts):
        for q in dsts:
            d = q - (r - 2)
            act(("ce", tk), "a%d" % d, T.junl[:, C * d:C * d + 127], T.ce[:, 0:127], F.Sign,
                bias=thr[:, d:d + 1], scale=-1.0, accum_out=one["a%d" % d])

    def lists(dsts, lf, name):
        for i, q in enumerate(dsts):
            d = q - (r - 2)
            act(("ik2", "a%d" % d), name + "f", lf[:, 5 * i:5 * i + 5], T.ik2[:, 0:5], bias=one["a%d" % d])

    def clamp(k, lf, ls, name):
        do("v", V.tensor_scalar, (name + "f",), name, ls[:, 0:5 * k], lf[:, 0:5 * k], 0.5, 127.0, A.mult, A.min)

    def pick(k, dst, ls, name, *keys):
        do("v", V.tensor_copy, ("xc", name) + keys, name + "c", dst.bitcast(dt.uint32),
           T.xc[:, 0:C + DS * len(keys)].bitcast(dt.uint32).indirect(ls[:, 0:5 * k]))

    def picks(k, dst, ls, name, *keys):
        act(("xcs", name) + keys, name + "s", dst, T.xcs[:, 0:C + DS * len(keys)].indirect(ls[:, 0:5 * k]), F.Copy)
    ka, kb = len(hop), len(dr)
    counts(dr[:1])
    for i, q in enumerate(hop):
        a = "a%d" % (q - (r - 2))
        do("v", V.tensor_scalar, ("ik2", a), "la", T.lsa[:, 5 * i:5 * i + 5], T.ik2[:, 0:5], one[a], 0.5, A.add, A.mult)
    pick(ka, T.spa[:, 0:DS * ka], T.lsa, "la", "xpad")
    picks(ka, T.spas[:, 0:DS * ka], T.lsa, "la", "xpad")
    relay = [(me["X"], chip), (me["Y"], chipy)]
    need("g", "lac")
    nls += send([(c, es, codes(T.rcb[:]), codes(T.spa[:, DS * i:DS * i + DS])) for i, (c, es) in enumerate(relay[:ka])], "rc")
    need("g", "las")
    nls += send([(c, es, T.rsb[:], T.spas[:, DS * i:DS * i + DS]) for i, (c, es) in enumerate(relay[:ka])], "rsc")
    counts(dr[1:])
    lists(dr, T.lfb, "lb")
    counts([r])
    lists([r], T.lfo, "lo")
    act(("prx",), "ia", T.junp[:, 0:n - 1], T.prx[:, 8:8 * (n - 1) + 1:8], F.Sign, scale=-1.0, bias=SH + 0.5, accum_out=one["ia"])

    do("v", V.tensor_copy, ("m2", "l2own"), "wi", T.wi[:, 0:4 * n], T.l2[:, 0:4 * n])
    wi = T.wi[:, 0:4 * n]
    do("v", V.tensor_scalar, ("wi",), "dei", T.dei[:, 1:m:2], wi, 127, None, A.bitwise_and)
    do("v", V.tensor_scalar, ("wi",), "dei2", T.dei[:, 0:m:2], wi, 8, 127, A.logical_shift_right, A.bitwise_and)
    do("v", V.tensor_scalar, ("wi",), "fli", T.fli[:, 1:m:2], wi, 7, 1, A.logical_shift_right, A.bitwise_and)
    do("v", V.tensor_scalar, ("wi",), "fli2", T.fli[:, 0:m:2], wi, 15, None, A.logical_shift_right)
    do("v", V.tensor_tensor, ("dei2", "prx"), "def_", T.def_[:, 0:m], T.dei[:, 0:m], T.prx[:, 0:m], A.add)
    do("v", V.tensor_tensor, ("fli2", "di"), "fd", T.fd[:, 0:m], T.fli[:, 0:m], T.di[:, 0:m], A.mult)
    clamp(kb, T.lfb, T.lsb, "lb")
    do("v", V.tensor_tensor_scan, ("def_", "rst8"), "er", T.er[:, 0:m], T.rst8[:, 0:m], T.def_[:, 0:m], 0.0, A.mult, A.add)
    pick(kb, T.spb[:, 0:DS * kb], T.lsb, "lb")
    picks(kb, T.spbs[:, 0:DS * kb], T.lsb, "lb")
    need("g", "lbc")
    nls += send([(T.cores[q], direct_engines(i), codes(T.win[:, base(r, q):base(r, q) + DS]), codes(T.spb[:, DS * i:DS * i + DS]))
                 for i, q in enumerate(dr)], "dc")
    need("g", "lbs")
    nls += send([(T.cores[q], direct_engines(i), T.wins[:, base(r, q):base(r, q) + DS], T.spbs[:, DS * i:DS * i + DS])
                 for i, q in enumerate(dr)], "dsc")
    do("v", V.tensor_tensor, ("er", "fd"), "po", T.po[:, 0:m], T.er[:, 0:m], T.fd[:, 0:m], A.add)
    clamp(1, T.lfo, T.lso, "lo")
    do("v", V.tensor_copy, ("po",), "pos", T.pos[:, 0:m], T.po[:, 0:m])
    act(("ia",), "g0", T.g[:, 0:1], one["ia"], scale=DS / 2.0, bias=float(OFF + DS * (n - 1) // 2))

    do("v", V.tensor_copy, ("pos", "slots", "mr0"), "mr2", T.mr2[:].indirect(T.pos[:, 0:m]), T.slots[:, 0:16 * m])
    b = base(r, r)
    pick(1, T.win[:, b:b + DS], T.lso, "lo")
    picks(1, T.wins[:, b:b + DS], T.lso, "lo")
    do("v", V.tensor_scalar, ("mr2",), "mk", T.mk[:], T.mr2[:, SH:SH + P], 0.0, None, A.is_gt)
    do("v", V.tensor_tensor_scan, ("mk", "g0"), "g", T.g[:, 1:P], T.mk[:, 1:P], T.mr2[:, SH + 1:SH + P], T.g[:, 0:1], A.add, A.max)
    do("v", V.tensor_tensor_scan, ("g", "dg2"), "sgm", T.sgm[:], T.g[:], T.dg[:], BIG, A.min, A.max)
    do("v", V.tensor_tensor, ("sgm",), "mn", T.mn[:], T.sgm[:, 14:256:16], T.sgm[:, 15:256:16], A.min)
    do("v", V.tensor_copy, ("mn",), "fin", T.fin[:], T.mn[:])

    for b in (0, 1):
        do("v", V.tensor_copy, ("dc", "loc", "fin"), "t%d" % b, T.t2[:, 128 * b:128 * b + 128].bitcast(dt.uint32),
           T.win[:].bitcast(dt.uint32).indirect(T.fin[:, 8 * b:8 * b + 8]))
        act(("dsc", "los", "fin"), "t%ds" % b, T.t2s[:, 128 * b:128 * b + 128],
            T.wins[:].indirect(T.fin[:, 8 * b:8 * b + 8]), F.Copy)
    for b in (0, 1):
        for o in (0, 1):
            k = 2 * b + o
            do("t", g.tensor.matmul_mx, ("wq", "t%d" % b, "t%ds" % b), "mm%d" % k, T.ps[:, 512 * k:512 * k + 128],
               T.wq[:, 128 * k:128 * k + 128], T.ws[:, 128 * k:128 * k + 128],
               T.t2[:, 128 * b:128 * b + 128], T.t2s[:, 128 * b:128 * b + 128], True, True)
    for b in (0, 1):
        do("v", V.tensor_copy, ("mm%d" % (2 * b),), "y0", T.ysb[:, 128 * b:128 * b + 128], T.ps[:, 1024 * b:1024 * b + 128])
        act(("mm%d" % (2 * b + 1),), "y1", T.ysb[:, P + 128 * b:P + 128 * b + 128], T.ps[:, 1024 * b + 512:1024 * b + 640], F.Copy)
    dma("y", ("y0", "y1"), "st0", "st0", T.y[:], T.ysb[:])

    for q, s in own.items():
        ev["end_" + q] = (s, count[q])
    for s, v in final.items():
        ev["end_" + s] = (s, v)
    ev["end_ls"] = ("ls", nls)
    need("g", *[k for k in ev if k.startswith("end_") or k.startswith("m1_")], "m2", "dc", "dsc")
